import numpy as np
import ml_dtypes


def mxq(x, axis, fmt="e4m3"):
    dtype, down = {"e4m3": (ml_dtypes.float8_e4m3fn, 7), "e5m2": (ml_dtypes.float8_e5m2, 14)}[fmt]
    v = np.moveaxis(np.asarray(x, np.float32).astype(ml_dtypes.bfloat16).astype(np.float64), axis, -1)
    blocks = v.reshape(v.shape[:-1] + (-1, 32))
    amax = np.abs(blocks).max(-1, keepdims=True)
    byte = np.maximum(np.where(amax > 0, np.frexp(amax)[1] - 1 + 127, 0) - down, 1)
    scale = np.exp2(byte - 127.0)
    codes = (blocks / scale).astype(np.float32).astype(dtype).astype(np.float64)
    return np.moveaxis((codes * scale).reshape(v.shape), -1, axis)


WIDE = False


def mx_kscale(k):
    if not WIDE:
        return np.ones(k)
    levels = np.array([10, -10, 5, -5, 0])
    if k % 512:
        return np.exp2(np.random.permutation(np.resize(levels, k // 32))).repeat(32)
    a = np.empty((k // 512, 16))
    for p in range(k // 512):
        a[p, :8] = np.random.permutation(np.resize(levels, 8))
        for g in range(8):
            far = levels[np.abs(levels - a[p, g]) >= 10]
            a[p, g + 8] = far[np.random.randint(len(far))]
    return np.exp2(a.ravel()).repeat(32)


def f64(x):
    return np.asarray(x).astype(np.float64)


def striped(idx):
    return np.tile(idx.reshape(-1, 16).T, (8, 1)).astype(np.uint16)


def unstriped(offs):
    return offs[:16].T.reshape(-1).astype(np.int64)


def striped8(idx):
    return np.concatenate([x.reshape(-1, 16).T for x in idx]).astype(np.uint16)


def runs(offs, k):
    lists = np.stack([offs[16 * r : 16 * r + 16].T.reshape(-1) for r in range(8)]).astype(np.int64)
    return lists[np.arange(k) % 512 // 64]


def pack_weight(w):
    k, n = w.shape
    w = f64(np.asarray(w, np.float32).astype(ml_dtypes.bfloat16)).reshape(k // 32, 32, n)
    amax = np.abs(w).max(1)
    byte = np.clip(np.where(amax > 0, np.frexp(amax)[1] - 1 + 127 - 7, 1), 1, 254)
    scaled = (w * np.exp2(127.0 - byte)[:, None, :]).reshape(k, n).astype(np.float32)
    words = np.ascontiguousarray(scaled.reshape(k // 512, 128, 4, n).transpose(0, 1, 3, 2)).astype(ml_dtypes.float8_e4m3fn).view(np.uint8)
    return words, np.ascontiguousarray(byte.astype(np.uint8).reshape(k // 512, 16, n))


def unpack_weight(words, scales):
    g, p, n, _ = words.shape
    vals = np.ascontiguousarray(words).view(ml_dtypes.float8_e4m3fn).astype(np.float64) * np.repeat(np.exp2(scales.astype(np.float64) - 127.0), 8, axis=1)[..., None]
    return vals.transpose(0, 1, 3, 2).reshape(g * 512, n)


K, T, S, N, U = 512, 2048, 512, 512, 1024


def setup_inputs():
    n = np.random.standard_normal
    s = mx_kscale(K)[:, None]
    packed_xT = pack_weight(n((K, T)) * s)
    return {
        "x_words": packed_xT[0],
        "x_scales": packed_xT[1],
        "w1": (n((K, N)) / np.sqrt(K) / s).astype(np.float32),
        "tab": n((N, U)).astype(np.float32),
        "offs": striped(np.random.permutation(T)[:S]),
        "rel": striped8(np.random.randint(0, U, (8, S))),
    }


def reference(x_words, x_scales, w1, tab, offs, rel):
    xq = unpack_weight(x_words, x_scales)[:, unstriped(offs)]
    y = mxq(f64(w1), 0, "e4m3").T @ xq
    p = y + f64(tab)[np.arange(N)[:, None], runs(rel, N)]
    e = np.exp(p - p.max(axis=1, keepdims=True))
    return e / e.sum(axis=1, keepdims=True)

@@ -1,0 +1,131 @@
+from contextlib import ExitStack
+
+import concourse.mybir as mybir
+
+K, T, S, N, U = 512, 2048, 512, 512, 1024
+FLOPS = 2 * K * N * S
+
+F32 = mybir.dt.float32
+BF16 = mybir.dt.bfloat16
+I32 = mybir.dt.int32
+U32 = mybir.dt.uint32
+U16 = mybir.dt.uint16
+U8 = mybir.dt.uint8
+FP8X4 = mybir.dt.float8_e4m3fn_x4
+ALU = mybir.AluOpType
+ACT = mybir.ActivationFunctionType
+AX = mybir.AxisListType
+
+P = 128
+PACK = 4
+BLOCKS = N // P
+HALF = BLOCKS // 2
+
+
+def tile_picked_relbias_none_p_kernel(tc, x_words, x_scales, w1, tab, offs, rel, out):
+    nc = tc.nc
+    with ExitStack() as ctx:
+        keep = ctx.enter_context(tc.tile_pool(name="keep", bufs=1))
+        psum = ctx.enter_context(tc.psum_pool(name="psum", bufs=1))
+
+        offs_sb = keep.tile([P, S // 16], U16, name="offs_sb")
+        rel_sb = keep.tile([P, S // 16], U16, name="rel_sb")
+        scale_table = keep.tile([P, T], U8, name="scale_table", align_bytes=64)
+        word_table = keep.tile([P, T], I32, name="word_table", align_bytes=64)
+        w_raw = keep.tile([P, PACK, N], F32, name="w_raw", align_bytes=64)
+        tabs = [keep.tile([P, U], F32, name=f"tab{b}", align_bytes=64) for b in range(BLOCKS)]
+
+        nc.vector.memset(scale_table[:].bitcast(I32), 0)
+        warm = keep.tile([P, 2], F32, name="warm")
+        nc.gpsimd.memset(warm[:, 0:1], 0.0)
+        nc.scalar.activation(warm[:, 1:2], warm[:, 0:1], ACT.Exp)
+        nc.sync.dma_start(offs_sb[:], offs)
+        scale_rows = x_scales[0].bitcast(I32)
+        w_rows = w1.rearrange("(p j) c -> p j c", j=PACK)
+        nc.sync.dma_start(w_raw[:, 0:2, :], w_rows[:, 0:2, :])
+        for q in range(4):
+            nc.sync.dma_start(scale_table[32 * q : 32 * q + 4, :].bitcast(I32), scale_rows[4 * q : 4 * q + 4, :])
+        nc.sync.dma_start(w_raw[:, 2:4, :], w_rows[:, 2:4, :])
+        nc.sync.dma_start(word_table[:], x_words[0].rearrange("p c r -> p (c r)").bitcast(I32))
+        nc.sync.dma_start(rel_sb[:], rel)
+        tab_rows = tab.rearrange("(p b) u -> b p u", b=BLOCKS)
+        out_rows = out.rearrange("(p b) s -> b p s", b=BLOCKS)
+        for b in range(BLOCKS):
+            nc.sync.dma_start(tabs[b][:], tab_rows[b])
+
+        x_bytes = keep.tile([P, S], U8, name="x_bytes", align_bytes=64)
+        nc.vector.tensor_copy(x_bytes[:], scale_table[:].indirect(offs_sb[:]))
+
+        w_view = w_raw[:].rearrange("p j (m b) -> p m b j", b=BLOCKS)
+        w_codes, w_bytes = [], []
+        for h in range(2):
+            grouped = keep.tile([P, HALF, P, PACK], BF16, name=f"grouped{h}", align_bytes=64)
+            dst = grouped[:].rearrange("p b m j -> p m b j")
+            src = w_view[:, :, HALF * h : HALF * (h + 1), :]
+            if h == 0:
+                nc.vector.tensor_copy(dst, src)
+            else:
+                nc.scalar.activation(dst, src, ACT.Copy)
+            codes = keep.tile([P, HALF * P], U32, name=f"w_codes{h}", align_bytes=64)
+            scales = keep.tile([P, HALF * P], U8, name=f"w_bytes{h}", align_bytes=64)
+            nc.vector.quantize_mx(out=codes[:].bitcast(FP8X4), scales=scales[:], in_=grouped[:].rearrange("p b m j -> p (b m j)"))
+            w_codes.append(codes)
+            w_bytes.append(scales)
+
+        x_codes = keep.tile([P, S], U32, name="x_codes", align_bytes=64)
+        nc.vector.tensor_copy(x_codes[:], word_table[:].bitcast(U32).indirect(offs_sb[:]))
+
+        scores, sides = [], []
+        for b in range(BLOCKS):
+            h, cols = b // HALF, slice(P * (b % HALF), P * (b % HALF + 1))
+            bank = psum.tile([P, S], F32, name=f"scores{b}")
+            nc.tensor.matmul_mx(
+                out=bank[:],
+                lhsT=w_codes[h][:, cols].bitcast(FP8X4),
+                lhsT_scale=w_bytes[h][:, cols],
+                rhs=x_codes[:].bitcast(FP8X4),
+                rhs_scale=x_bytes[:],
+                start=True,
+                stop=True,
+            )
+            scores.append(bank)
+            side = keep.tile([P, S], F32, name=f"side{b}")
+            if b > 0:
+                nc.scalar.copy(side[:], bank[:])
+            sides.append(side)
+
+        def add_bias(b):
+            logits = keep.tile([P, S], F32, name=f"logits{b}")
+            if b == 0:
+                nc.vector.tensor_copy(sides[b][:], tabs[b][:].indirect(rel_sb[:]))
+                nc.vector.tensor_tensor(logits[:], scores[b][:], sides[b][:], ALU.add)
+            else:
+                nc.vector.tensor_tensor(logits[:], tabs[b][:].indirect(rel_sb[:]), sides[b][:], ALU.add)
+            return logits
+
+        def exponentiate(b, logits):
+            stats = keep.tile([P, 2], F32, name="stats")
+            neg_max, total = stats[:, 0:1], stats[:, 1:2]
+            nc.vector.tensor_reduce(neg_max, logits[:], AX.X, ALU.max, negate=True)
+            expd = keep.tile([P, S], F32, name=f"expd{b}")
+            nc.scalar.activation(expd[:], logits[:], ACT.Exp, bias=neg_max, scale=1.0, accum_out=total)
+            return expd, total
+
+        def normalise(b, expd, total):
+            last = b == BLOCKS - 1
+            inverse = sides[b if last else b + 1][:, 0:1]
+            nc.vector.reciprocal(inverse, total)
+            result = keep.tile([P, S], F32, name=f"result{b}")
+            if last:
+                nc.vector.tensor_scalar(result[:], expd[:], inverse, None, ALU.mult)
+            else:
+                nc.scalar.activation(result[:], expd[:], ACT.Copy, scale=inverse)
+            nc.sync.dma_start(out_rows[b], result[:])
+
+        pending = None
+        for b in range(BLOCKS):
+            logits = add_bias(b)
+            if pending is not None:
+                normalise(b - 1, *pending)
+            pending = exponentiate(b, logits)
+        normalise(BLOCKS - 1, *pending)

@@ -39,12 +39,12 @@ def tile_picked_relbias_none_p_kernel(tc, x_words, x_scales, w1, tab, offs, rel,
         warm = keep.tile([P, 2], F32, name="warm")
         nc.gpsimd.memset(warm[:, 0:1], 0.0)
         nc.scalar.activation(warm[:, 1:2], warm[:, 0:1], ACT.Exp)
-        nc.sync.dma_start(offs_sb[:], offs)
         scale_rows = x_scales[0].bitcast(I32)
         w_rows = w1.rearrange("(p j) c -> p j c", j=PACK)
         nc.sync.dma_start(w_raw[:, 0:2, :], w_rows[:, 0:2, :])
-        for q in range(4):
-            nc.sync.dma_start(scale_table[32 * q : 32 * q + 4, :].bitcast(I32), scale_rows[4 * q : 4 * q + 4, :])
+        nc.sync.dma_start(offs_sb[:], offs)
+        for r in range(4):
+            nc.sync.dma_start(scale_table[r:P:32, :].bitcast(I32), scale_rows[r:16:4, :])
         nc.sync.dma_start(w_raw[:, 2:4, :], w_rows[:, 2:4, :])
         nc.sync.dma_start(word_table[:], x_words[0].rearrange("p c r -> p (c r)").bitcast(I32))
         nc.sync.dma_start(rel_sb[:], rel)
@@ -73,59 +73,81 @@ def tile_picked_relbias_none_p_kernel(tc, x_words, x_scales, w1, tab, offs, rel,
             w_bytes.append(scales)
 
         x_codes = keep.tile([P, S], U32, name="x_codes", align_bytes=64)
-        nc.vector.tensor_copy(x_codes[:], word_table[:].bitcast(U32).indirect(offs_sb[:]))
+        for k in range(2):
+            nc.vector.tensor_copy(x_codes[:, 256 * k : 256 * (k + 1)], word_table[:].bitcast(U32).indirect(offs_sb[:, 16 * k : 16 * (k + 1)]))
 
-        scores, sides = [], []
-        for b in range(BLOCKS):
+        scores = [psum.tile([P, S], F32, name=f"scores{b}") for b in range(BLOCKS)]
+
+        def score(b, keys):
             h, cols = b // HALF, slice(P * (b % HALF), P * (b % HALF + 1))
-            bank = psum.tile([P, S], F32, name=f"scores{b}")
             nc.tensor.matmul_mx(
-                out=bank[:],
+                out=scores[b][:, keys],
                 lhsT=w_codes[h][:, cols].bitcast(FP8X4),
                 lhsT_scale=w_bytes[h][:, cols],
-                rhs=x_codes[:].bitcast(FP8X4),
-                rhs_scale=x_bytes[:],
+                rhs=x_codes[:, keys].bitcast(FP8X4),
+                rhs_scale=x_bytes[:, keys],
                 start=True,
                 stop=True,
             )
-            scores.append(bank)
-            side = keep.tile([P, S], F32, name=f"side{b}")
-            if b > 0:
-                nc.scalar.copy(side[:], bank[:])
-            sides.append(side)
+
+        for keys in (slice(0, 256), slice(256, 512)):
+            score(1, keys)
+            score(0, keys)
+        score(2, slice(0, S))
+        score(3, slice(0, S))
+
+        sides, logits, expd, totals = {}, {}, {}, {}
+
+        def leave_bank(b, tag):
+            sides[b] = keep.tile([P, S], F32, name=tag)
+            nc.scalar.copy(sides[b][:], scores[b][:])
 
         def add_bias(b):
-            logits = keep.tile([P, S], F32, name=f"logits{b}")
-            if b == 0:
-                nc.vector.tensor_copy(sides[b][:], tabs[b][:].indirect(rel_sb[:]))
-                nc.vector.tensor_tensor(logits[:], scores[b][:], sides[b][:], ALU.add)
-            else:
-                nc.vector.tensor_tensor(logits[:], tabs[b][:].indirect(rel_sb[:]), sides[b][:], ALU.add)
-            return logits
+            logits[b] = keep.tile([P, S], F32, name=f"logits{b}")
+            nc.vector.tensor_tensor(logits[b][:], tabs[b][:].indirect(rel_sb[:]), sides[b][:], ALU.add)
 
-        def exponentiate(b, logits):
-            stats = keep.tile([P, 2], F32, name="stats")
-            neg_max, total = stats[:, 0:1], stats[:, 1:2]
-            nc.vector.tensor_reduce(neg_max, logits[:], AX.X, ALU.max, negate=True)
-            expd = keep.tile([P, S], F32, name=f"expd{b}")
-            nc.scalar.activation(expd[:], logits[:], ACT.Exp, bias=neg_max, scale=1.0, accum_out=total)
-            return expd, total
+        def exponentiate(b):
+            neg_max = keep.tile([P, 1], F32, name=f"neg_max{b}")
+            nc.vector.tensor_reduce(neg_max[:], logits[b][:], AX.X, ALU.max, negate=True)
+            expd[b] = keep.tile([P, S], F32, name=f"expd{b}")
+            totals[b] = keep.tile([P, 1], F32, name=f"total{b}")
+            nc.scalar.activation(expd[b][:], logits[b][:], ACT.Exp, bias=neg_max[:], scale=1.0, accum_out=totals[b][:])
 
-        def normalise(b, expd, total):
-            last = b == BLOCKS - 1
-            inverse = sides[b if last else b + 1][:, 0:1]
-            nc.vector.reciprocal(inverse, total)
+        def invert(b):
+            inverse = keep.tile([P, 1], F32, name=f"inverse{b}")
+            nc.vector.reciprocal(inverse[:], totals[b][:])
+            return inverse[:]
+
+        def normalise(b, inverse, on_vector):
             result = keep.tile([P, S], F32, name=f"result{b}")
-            if last:
-                nc.vector.tensor_scalar(result[:], expd[:], inverse, None, ALU.mult)
+            if on_vector:
+                nc.vector.tensor_scalar(result[:], expd[b][:], inverse, None, ALU.mult)
             else:
-                nc.scalar.activation(result[:], expd[:], ACT.Copy, scale=inverse)
+                nc.scalar.activation(result[:], expd[b][:], ACT.Copy, scale=inverse)
             nc.sync.dma_start(out_rows[b], result[:])
 
-        pending = None
-        for b in range(BLOCKS):
-            logits = add_bias(b)
-            if pending is not None:
-                normalise(b - 1, *pending)
-            pending = exponentiate(b, logits)
-        normalise(BLOCKS - 1, *pending)
+        leave_bank(1, "side1")
+        leave_bank(2, "side2")
+        sides[0] = keep.tile([P, S], F32, name="side0")
+        nc.vector.tensor_copy(sides[0][:], tabs[0][:].indirect(rel_sb[:]))
+        logits[0] = keep.tile([P, S], F32, name="logits0")
+        nc.vector.tensor_tensor(logits[0][:], scores[0][:], sides[0][:], ALU.add)
+        add_bias(1)
+        exponentiate(0)
+        exponentiate(1)
+        add_bias(2)
+        leave_bank(3, "logits0")
+        normalise(0, invert(0), False)
+        exponentiate(2)
+        normalise(1, invert(1), False)
+        add_bias(3)
+        inverse2 = invert(2)
+        exponentiate(3)
+        normalise(2, inverse2, True)
+        inverse = invert(3)
+        left = keep.tile([P, 256], F32, name="left")
+        right = keep.tile([P, 256], F32, name="right")
+        nc.vector.tensor_scalar(left[:], expd[3][:, 0:256], inverse, None, ALU.mult)
+        nc.sync.dma_start(out_rows[3][:, 0:256], left[:])
+        nc.scalar.activation(right[:], expd[3][:, 256:512], ACT.Copy, scale=inverse)
+        nc.scalar.dma_start(out_rows[3][:, 256:512], right[:])

@@ -20,6 +20,9 @@ P = 128
 PACK = 4
 BLOCKS = N // P
 HALF = BLOCKS // 2
+KEYS_A, KEYS_B = slice(0, S // 2), slice(S // 2, S)
+CAST_SPLIT = 88
+TAIL_SPLIT = 256
 
 
 def tile_picked_relbias_none_p_kernel(tc, x_words, x_scales, w1, tab, offs, rel, out):
@@ -37,7 +40,7 @@ def tile_picked_relbias_none_p_kernel(tc, x_words, x_scales, w1, tab, offs, rel,
 
         nc.vector.memset(scale_table[:].bitcast(I32), 0)
         warm = keep.tile([P, 2], F32, name="warm")
-        nc.gpsimd.memset(warm[:, 0:1], 0.0)
+        nc.vector.memset(warm[:, 0:1], 0.0)
         nc.scalar.activation(warm[:, 1:2], warm[:, 0:1], ACT.Exp)
         scale_rows = x_scales[0].bitcast(I32)
         w_rows = w1.rearrange("(p j) c -> p j c", j=PACK)
@@ -50,25 +53,26 @@ def tile_picked_relbias_none_p_kernel(tc, x_words, x_scales, w1, tab, offs, rel,
         nc.sync.dma_start(rel_sb[:], rel)
         tab_rows = tab.rearrange("(p b) u -> b p u", b=BLOCKS)
         out_rows = out.rearrange("(p b) s -> b p s", b=BLOCKS)
-        for b in range(BLOCKS):
+        for b in range(len(tabs)):
             nc.sync.dma_start(tabs[b][:], tab_rows[b])
 
         x_bytes = keep.tile([P, S], U8, name="x_bytes", align_bytes=64)
         nc.vector.tensor_copy(x_bytes[:], scale_table[:].indirect(offs_sb[:]))
 
-        w_view = w_raw[:].rearrange("p j (m b) -> p m b j", b=BLOCKS)
+        grouped = keep.tile([P, BLOCKS, P, PACK], BF16, name="grouped", align_bytes=64)
+        dst = grouped[:].rearrange("p b m j -> p m b j")
+        src = w_raw[:].rearrange("p j (m b) -> p m b j", b=BLOCKS)
+        nc.vector.tensor_copy(dst[:, 0:CAST_SPLIT], src[:, 0:CAST_SPLIT])
+        nc.scalar.activation(dst[:, CAST_SPLIT:P], src[:, CAST_SPLIT:P], ACT.Copy)
         w_codes, w_bytes = [], []
         for h in range(2):
-            grouped = keep.tile([P, HALF, P, PACK], BF16, name=f"grouped{h}", align_bytes=64)
-            dst = grouped[:].rearrange("p b m j -> p m b j")
-            src = w_view[:, :, HALF * h : HALF * (h + 1), :]
-            if h == 0:
-                nc.vector.tensor_copy(dst, src)
-            else:
-                nc.scalar.activation(dst, src, ACT.Copy)
             codes = keep.tile([P, HALF * P], U32, name=f"w_codes{h}", align_bytes=64)
             scales = keep.tile([P, HALF * P], U8, name=f"w_bytes{h}", align_bytes=64)
-            nc.vector.quantize_mx(out=codes[:].bitcast(FP8X4), scales=scales[:], in_=grouped[:].rearrange("p b m j -> p (b m j)"))
+            nc.vector.quantize_mx(
+                out=codes[:].bitcast(FP8X4),
+                scales=scales[:],
+                in_=grouped[:, HALF * h : HALF * (h + 1)].rearrange("p b m j -> p (b m j)"),
+            )
             w_codes.append(codes)
             w_bytes.append(scales)
 
@@ -76,12 +80,11 @@ def tile_picked_relbias_none_p_kernel(tc, x_words, x_scales, w1, tab, offs, rel,
         for k in range(2):
             nc.vector.tensor_copy(x_codes[:, 256 * k : 256 * (k + 1)], word_table[:].bitcast(U32).indirect(offs_sb[:, 16 * k : 16 * (k + 1)]))
 
-        scores = [psum.tile([P, S], F32, name=f"scores{b}") for b in range(BLOCKS)]
-
-        def score(b, keys):
+        def score(b, keys, bank):
             h, cols = b // HALF, slice(P * (b % HALF), P * (b % HALF + 1))
+            scores = psum.tile([P, keys.stop - keys.start], F32, name=bank)
             nc.tensor.matmul_mx(
-                out=scores[b][:, keys],
+                out=scores[:],
                 lhsT=w_codes[h][:, cols].bitcast(FP8X4),
                 lhsT_scale=w_bytes[h][:, cols],
                 rhs=x_codes[:, keys].bitcast(FP8X4),
@@ -89,25 +92,24 @@ def tile_picked_relbias_none_p_kernel(tc, x_words, x_scales, w1, tab, offs, rel,
                 start=True,
                 stop=True,
             )
+            return scores
 
-        for keys in (slice(0, 256), slice(256, 512)):
-            score(1, keys)
-            score(0, keys)
-        score(2, slice(0, S))
-        score(3, slice(0, S))
+        staged = [keep.tile([P, S // 2 if b == 0 else S], F32, name=f"staged{b}") for b in range(BLOCKS)]
+        logits = [keep.tile([P, S], F32, name=f"logits{b}", align_bytes=64) for b in range(BLOCKS)]
+        expd, totals = {}, {}
 
-        sides, logits, expd, totals = {}, {}, {}, {}
-
-        def leave_bank(b, tag):
-            sides[b] = keep.tile([P, S], F32, name=tag)
-            nc.scalar.copy(sides[b][:], scores[b][:])
+        nc.scalar.copy(staged[0][:], score(0, KEYS_A, "bank0a")[:])
+        nc.scalar.copy(staged[1][:, KEYS_A], score(1, KEYS_A, "bank1a")[:])
+        scores0b = score(0, KEYS_B, "bank0b")
+        nc.scalar.copy(staged[1][:, KEYS_B], score(1, KEYS_B, "bank1b")[:])
+        nc.scalar.copy(staged[2][:], score(2, slice(0, S), "bank2")[:])
+        nc.scalar.copy(staged[3][:], score(3, slice(0, S), "bank3")[:])
 
         def add_bias(b):
-            logits[b] = keep.tile([P, S], F32, name=f"logits{b}")
-            nc.vector.tensor_tensor(logits[b][:], tabs[b][:].indirect(rel_sb[:]), sides[b][:], ALU.add)
+            nc.vector.tensor_tensor(logits[b][:], tabs[b][:].indirect(rel_sb[:]), staged[b][:], ALU.add)
 
-        def exponentiate(b):
-            neg_max = keep.tile([P, 1], F32, name=f"neg_max{b}")
+        def exponentiate(b, tag):
+            neg_max = keep.tile([P, 1], F32, name=tag, align_bytes=64)
             nc.vector.tensor_reduce(neg_max[:], logits[b][:], AX.X, ALU.max, negate=True)
             expd[b] = keep.tile([P, S], F32, name=f"expd{b}")
             totals[b] = keep.tile([P, 1], F32, name=f"total{b}")
@@ -126,28 +128,24 @@ def tile_picked_relbias_none_p_kernel(tc, x_words, x_scales, w1, tab, offs, rel,
                 nc.scalar.activation(result[:], expd[b][:], ACT.Copy, scale=inverse)
             nc.sync.dma_start(out_rows[b], result[:])
 
-        leave_bank(1, "side1")
-        leave_bank(2, "side2")
-        sides[0] = keep.tile([P, S], F32, name="side0")
-        nc.vector.tensor_copy(sides[0][:], tabs[0][:].indirect(rel_sb[:]))
-        logits[0] = keep.tile([P, S], F32, name="logits0")
-        nc.vector.tensor_tensor(logits[0][:], scores[0][:], sides[0][:], ALU.add)
+        bias0b = keep.tile([P, S // 2], F32, name="bias0b")
+        nc.vector.tensor_copy(bias0b[:], tabs[0][:].indirect(rel_sb[:, 16:32]))
+        nc.vector.tensor_tensor(logits[0][:, KEYS_A], tabs[0][:].indirect(rel_sb[:, 0:16]), staged[0][:], ALU.add)
+        nc.vector.tensor_tensor(logits[0][:, KEYS_B], scores0b[:], bias0b[:], ALU.add)
         add_bias(1)
-        exponentiate(0)
-        exponentiate(1)
+        exponentiate(0, "neg_max")
         add_bias(2)
-        leave_bank(3, "logits0")
         normalise(0, invert(0), False)
-        exponentiate(2)
-        normalise(1, invert(1), False)
+        exponentiate(1, "neg_max")
         add_bias(3)
-        inverse2 = invert(2)
-        exponentiate(3)
-        normalise(2, inverse2, True)
+        normalise(1, invert(1), False)
+        exponentiate(2, "neg_max")
+        exponentiate(3, "logits1")
+        normalise(2, invert(2), True)
         inverse = invert(3)
-        left = keep.tile([P, 256], F32, name="left")
-        right = keep.tile([P, 256], F32, name="right")
-        nc.vector.tensor_scalar(left[:], expd[3][:, 0:256], inverse, None, ALU.mult)
-        nc.sync.dma_start(out_rows[3][:, 0:256], left[:])
-        nc.scalar.activation(right[:], expd[3][:, 256:512], ACT.Copy, scale=inverse)
-        nc.scalar.dma_start(out_rows[3][:, 256:512], right[:])
+        left = keep.tile([P, TAIL_SPLIT], F32, name="left")
+        right = keep.tile([P, S - TAIL_SPLIT], F32, name="right")
+        nc.vector.tensor_scalar(left[:], expd[3][:, 0:TAIL_SPLIT], inverse, None, ALU.mult)
+        nc.sync.dma_start(out_rows[3][:, 0:TAIL_SPLIT], left[:])
+        nc.scalar.activation(right[:], expd[3][:, TAIL_SPLIT:S], ACT.Copy, scale=inverse)
+        nc.scalar.dma_start(out_rows[3][:, TAIL_SPLIT:S], right[:])

@@ -36,28 +36,35 @@ def tile_picked_relbias_none_p_kernel(tc, x_words, x_scales, w1, tab, offs, rel,
         scale_table = keep.tile([P, T], U8, name="scale_table", align_bytes=64)
         word_table = keep.tile([P, T], I32, name="word_table", align_bytes=64)
         w_raw = keep.tile([P, PACK, N], F32, name="w_raw", align_bytes=64)
-        tabs = [keep.tile([P, U], F32, name=f"tab{b}", align_bytes=64) for b in range(BLOCKS)]
+        tabs = []
+        x_plane = keep.tile([P, S], U8, name="x_plane", align_bytes=64)
 
         nc.vector.memset(scale_table[:].bitcast(I32), 0)
+        nc.vector.memset(x_plane[:].bitcast(I32), 0)
         warm = keep.tile([P, 2], F32, name="warm")
         nc.vector.memset(warm[:, 0:1], 0.0)
         nc.scalar.activation(warm[:, 1:2], warm[:, 0:1], ACT.Exp)
         scale_rows = x_scales[0].bitcast(I32)
         w_rows = w1.rearrange("(p j) c -> p j c", j=PACK)
-        nc.sync.dma_start(w_raw[:, 0:2, :], w_rows[:, 0:2, :])
+        nc.sync.dma_start(w_raw[:, 0:1, :], w_rows[:, 0:1, :])
         nc.sync.dma_start(offs_sb[:], offs)
-        for r in range(4):
-            nc.sync.dma_start(scale_table[r:P:32, :].bitcast(I32), scale_rows[r:16:4, :])
-        nc.sync.dma_start(w_raw[:, 2:4, :], w_rows[:, 2:4, :])
+        nc.sync.dma_start(scale_table[0:P:8, :].bitcast(I32), scale_rows)
+        nc.sync.dma_start(w_raw[:, 1:4, :], w_rows[:, 1:4, :])
         nc.sync.dma_start(word_table[:], x_words[0].rearrange("p c r -> p (c r)").bitcast(I32))
         nc.sync.dma_start(rel_sb[:], rel)
         tab_rows = tab.rearrange("(p b) u -> b p u", b=BLOCKS)
         out_rows = out.rearrange("(p b) s -> b p s", b=BLOCKS)
-        for b in range(len(tabs)):
-            nc.sync.dma_start(tabs[b][:], tab_rows[b])
+
+        def load_tab(b, tag):
+            table = keep.tile([P, U], F32, name=tag, align_bytes=64)
+            nc.sync.dma_start(table[:], tab_rows[b])
+            tabs.append(table)
 
         x_bytes = keep.tile([P, S], U8, name="x_bytes", align_bytes=64)
         nc.vector.tensor_copy(x_bytes[:], scale_table[:].indirect(offs_sb[:]))
+        for r in range(4):
+            nc.sync.dma_start(x_plane[4 + r : P : 32, :].bitcast(I32), x_bytes[8 * r : P : 32, :].bitcast(I32))
+        load_tab(0, "scale_table")
 
         grouped = keep.tile([P, BLOCKS, P, PACK], BF16, name="grouped", align_bytes=64)
         dst = grouped[:].rearrange("p b m j -> p m b j")
@@ -76,9 +83,13 @@ def tile_picked_relbias_none_p_kernel(tc, x_words, x_scales, w1, tab, offs, rel,
             w_codes.append(codes)
             w_bytes.append(scales)
 
+        load_tab(1, "w_raw")
+        load_tab(2, "grouped")
+
         x_codes = keep.tile([P, S], U32, name="x_codes", align_bytes=64)
         for k in range(2):
             nc.vector.tensor_copy(x_codes[:, 256 * k : 256 * (k + 1)], word_table[:].bitcast(U32).indirect(offs_sb[:, 16 * k : 16 * (k + 1)]))
+        load_tab(3, "word_table")
 
         def score(b, keys, bank):
             h, cols = b // HALF, slice(P * (b % HALF), P * (b % HALF + 1))
@@ -88,20 +99,21 @@ def tile_picked_relbias_none_p_kernel(tc, x_words, x_scales, w1, tab, offs, rel,
                 lhsT=w_codes[h][:, cols].bitcast(FP8X4),
                 lhsT_scale=w_bytes[h][:, cols],
                 rhs=x_codes[:, keys].bitcast(FP8X4),
-                rhs_scale=x_bytes[:, keys],
+                rhs_scale=x_plane[4:P, keys],
                 start=True,
                 stop=True,
             )
             return scores
 
-        staged = [keep.tile([P, S // 2 if b == 0 else S], F32, name=f"staged{b}") for b in range(BLOCKS)]
+        staged = [keep.tile([P, S // 2 if b < HALF else S], F32, name=f"staged{b}", align_bytes=64) for b in range(BLOCKS)]
+        staged1b = keep.tile([P, S // 2], F32, name="staged1b")
         logits = [keep.tile([P, S], F32, name=f"logits{b}", align_bytes=64) for b in range(BLOCKS)]
         expd, totals = {}, {}
 
         nc.scalar.copy(staged[0][:], score(0, KEYS_A, "bank0a")[:])
-        nc.scalar.copy(staged[1][:, KEYS_A], score(1, KEYS_A, "bank1a")[:])
+        nc.scalar.copy(staged[1][:], score(1, KEYS_A, "bank1a")[:])
         scores0b = score(0, KEYS_B, "bank0b")
-        nc.scalar.copy(staged[1][:, KEYS_B], score(1, KEYS_B, "bank1b")[:])
+        nc.scalar.copy(staged1b[:], score(1, KEYS_B, "bank1b")[:])
         nc.scalar.copy(staged[2][:], score(2, slice(0, S), "bank2")[:])
         nc.scalar.copy(staged[3][:], score(3, slice(0, S), "bank3")[:])
 
@@ -132,14 +144,15 @@ def tile_picked_relbias_none_p_kernel(tc, x_words, x_scales, w1, tab, offs, rel,
         nc.vector.tensor_copy(bias0b[:], tabs[0][:].indirect(rel_sb[:, 16:32]))
         nc.vector.tensor_tensor(logits[0][:, KEYS_A], tabs[0][:].indirect(rel_sb[:, 0:16]), staged[0][:], ALU.add)
         nc.vector.tensor_tensor(logits[0][:, KEYS_B], scores0b[:], bias0b[:], ALU.add)
-        add_bias(1)
-        exponentiate(0, "neg_max")
+        nc.vector.tensor_tensor(logits[1][:, KEYS_A], tabs[1][:].indirect(rel_sb[:, 0:16]), staged[1][:], ALU.add)
+        nc.vector.tensor_tensor(logits[1][:, KEYS_B], tabs[1][:].indirect(rel_sb[:, 16:32]), staged1b[:], ALU.add)
+        exponentiate(0, "staged1")
         add_bias(2)
         normalise(0, invert(0), False)
-        exponentiate(1, "neg_max")
+        exponentiate(1, "staged1")
         add_bias(3)
         normalise(1, invert(1), False)
-        exponentiate(2, "neg_max")
+        exponentiate(2, "staged1")
         exponentiate(3, "logits1")
         normalise(2, invert(2), True)
         inverse = invert(3)

@@ -21,7 +21,7 @@ PACK = 4
 BLOCKS = N // P
 HALF = BLOCKS // 2
 KEYS_A, KEYS_B = slice(0, S // 2), slice(S // 2, S)
-CAST_SPLIT = 88
+CAST_SPLIT = 80
 TAIL_SPLIT = 256
 
 
@@ -66,11 +66,12 @@ def tile_picked_relbias_none_p_kernel(tc, x_words, x_scales, w1, tab, offs, rel,
             nc.sync.dma_start(x_plane[4 + r : P : 32, :].bitcast(I32), x_bytes[8 * r : P : 32, :].bitcast(I32))
         load_tab(0, "scale_table")
 
-        grouped = keep.tile([P, BLOCKS, P, PACK], BF16, name="grouped", align_bytes=64)
-        dst = grouped[:].rearrange("p b m j -> p m b j")
+        grouped = [keep.tile([P, HALF, P, PACK], BF16, name=f"grouped{h}", align_bytes=64) for h in range(2)]
+        dst = [grouped[h][:].rearrange("p b m j -> p m b j") for h in range(2)]
         src = w_raw[:].rearrange("p j (m b) -> p m b j", b=BLOCKS)
-        nc.vector.tensor_copy(dst[:, 0:CAST_SPLIT], src[:, 0:CAST_SPLIT])
-        nc.scalar.activation(dst[:, CAST_SPLIT:P], src[:, CAST_SPLIT:P], ACT.Copy)
+        nc.vector.tensor_copy(dst[0], src[:, :, 0:HALF])
+        nc.scalar.activation(dst[1][:, 0:CAST_SPLIT], src[:, 0:CAST_SPLIT, HALF:BLOCKS], ACT.Copy)
+        nc.vector.tensor_copy(dst[1][:, CAST_SPLIT:P], src[:, CAST_SPLIT:P, HALF:BLOCKS])
         w_codes, w_bytes = [], []
         for h in range(2):
             codes = keep.tile([P, HALF * P], U32, name=f"w_codes{h}", align_bytes=64)
@@ -78,13 +79,13 @@ def tile_picked_relbias_none_p_kernel(tc, x_words, x_scales, w1, tab, offs, rel,
             nc.vector.quantize_mx(
                 out=codes[:].bitcast(FP8X4),
                 scales=scales[:],
-                in_=grouped[:, HALF * h : HALF * (h + 1)].rearrange("p b m j -> p (b m j)"),
+                in_=grouped[h][:].rearrange("p b m j -> p (b m j)"),
             )
             w_codes.append(codes)
             w_bytes.append(scales)
 
         load_tab(1, "w_raw")
-        load_tab(2, "grouped")
+        load_tab(2, "grouped1")
 
         x_codes = keep.tile([P, S], U32, name="x_codes", align_bytes=64)
         for k in range(2):
@@ -154,7 +155,11 @@ def tile_picked_relbias_none_p_kernel(tc, x_words, x_scales, w1, tab, offs, rel,
         normalise(1, invert(1), False)
         exponentiate(2, "staged1")
         exponentiate(3, "logits1")
-        normalise(2, invert(2), True)
+        inverse2 = invert(2)
+        for name, keys in (("result2a", KEYS_A), ("result2b", KEYS_B)):
+            piece = keep.tile([P, S // 2], F32, name=name)
+            nc.vector.tensor_scalar(piece[:], expd[2][:, keys], inverse2, None, ALU.mult)
+            nc.sync.dma_start(out_rows[2][:, keys], piece[:])
         inverse = invert(3)
         left = keep.tile([P, TAIL_SPLIT], F32, name="left")
         right = keep.tile([P, S - TAIL_SPLIT], F32, name="right")

@@ -1,6 +1,7 @@
 from contextlib import ExitStack
 
 import concourse.mybir as mybir
+from concourse.masks import make_identity
 
 K, T, S, N, U = 512, 2048, 512, 512, 1024
 FLOPS = 2 * K * N * S
@@ -44,6 +45,9 @@ def tile_picked_relbias_none_p_kernel(tc, x_words, x_scales, w1, tab, offs, rel,
         warm = keep.tile([P, 2], F32, name="warm")
         nc.vector.memset(warm[:, 0:1], 0.0)
         nc.scalar.activation(warm[:, 1:2], warm[:, 0:1], ACT.Exp)
+        identity = keep.tile([P, P], F32, name="identity")
+        nc.vector.memset(identity[:], 0.0)
+        make_identity(nc, identity[:], nomemset=True)
         scale_rows = x_scales[0].bitcast(I32)
         w_rows = w1.rearrange("(p j) c -> p j c", j=PACK)
         nc.sync.dma_start(w_raw[:, 0:1, :], w_rows[:, 0:1, :])
@@ -106,17 +110,46 @@ def tile_picked_relbias_none_p_kernel(tc, x_words, x_scales, w1, tab, offs, rel,
             )
             return scores
 
-        staged = [keep.tile([P, S // 2 if b < HALF else S], F32, name=f"staged{b}", align_bytes=64) for b in range(BLOCKS)]
-        staged1b = keep.tile([P, S // 2], F32, name="staged1b")
-        logits = [keep.tile([P, S], F32, name=f"logits{b}", align_bytes=64) for b in range(BLOCKS)]
+        staged = [keep.tile([P, S if b % 2 else S // 2], F32, name=f"staged{b}", align_bytes=64) for b in range(BLOCKS)]
+        shared = keep.tile([P, S + S // 2], F32, name="shared", align_bytes=64)
+        logits = [keep.tile([P, S], F32, name="logits0", align_bytes=64), shared[:, S // 2 :], keep.tile([P, S], F32, name="logits2"), shared[:, :S]]
         expd, totals = {}, {}
 
         nc.scalar.copy(staged[0][:], score(0, KEYS_A, "bank0a")[:])
-        nc.scalar.copy(staged[1][:], score(1, KEYS_A, "bank1a")[:])
-        scores0b = score(0, KEYS_B, "bank0b")
-        nc.scalar.copy(staged1b[:], score(1, KEYS_B, "bank1b")[:])
-        nc.scalar.copy(staged[2][:], score(2, slice(0, S), "bank2")[:])
-        nc.scalar.copy(staged[3][:], score(3, slice(0, S), "bank3")[:])
+        nc.scalar.copy(staged[1][:, KEYS_A], score(1, KEYS_A, "bank1a")[:])
+        nc.scalar.copy(staged[1][:, KEYS_B], score(1, KEYS_B, "bank1b")[:])
+        scores0b = psum.tile([P, S // 2], F32, name="bank0b")
+        for k in range(2):
+            keys = slice(S // 2 + P * k, S // 2 + P * (k + 1))
+            nc.tensor.matmul_mx(
+                out=scores0b[:, P * k : P * (k + 1)],
+                lhsT=x_codes[:, keys].bitcast(FP8X4),
+                lhsT_scale=x_plane[4:P, keys],
+                rhs=w_codes[0][:, 0:P].bitcast(FP8X4),
+                rhs_scale=w_bytes[0][:, 0:P],
+                start=True,
+                stop=True,
+            )
+        bias0b = keep.tile([P, S // 2], F32, name="bias0b")
+        nc.vector.tensor_copy(bias0b[:], tabs[0][:].indirect(rel_sb[:, 16:32]))
+        turned = psum.tile([P, S // 2], F32, name="turned")
+        for k in range(2):
+            nc.tensor.transpose(turned[:, P * k : P * (k + 1)], bias0b[:, P * k : P * (k + 1)], identity[:])
+        scores2 = score(2, slice(0, S), "bank2")
+        staged2b = keep.tile([P, S // 2], F32, name="staged2b", align_bytes=64)
+        nc.scalar.copy(staged[2][:], scores2[:, KEYS_A])
+        staged0b = keep.tile([P, S // 2], F32, name="staged0b")
+        nc.scalar.copy(staged0b[:], scores0b[:])
+        turned_sb = keep.tile([P, S // 2], F32, name="turned_sb")
+        nc.scalar.copy(turned_sb[:], turned[:])
+        nc.scalar.copy(staged2b[:], scores2[:, KEYS_B])
+        back = psum.tile([P, S // 2], F32, name="back")
+        for k in range(2):
+            cols = slice(P * k, P * (k + 1))
+            nc.tensor.matmul(back[:, cols], staged0b[:, cols], identity[:], start=True, stop=False, is_transpose=True)
+            nc.tensor.matmul(back[:, cols], turned_sb[:, cols], identity[:], start=False, stop=True, is_transpose=True)
+        nc.scalar.copy(logits[0][:, KEYS_B], back[:])
+        nc.scalar.copy(staged[3][:], score(3, slice(0, S), "turned")[:])
 
         def add_bias(b):
             nc.vector.tensor_tensor(logits[b][:], tabs[b][:].indirect(rel_sb[:]), staged[b][:], ALU.add)
@@ -141,20 +174,18 @@ def tile_picked_relbias_none_p_kernel(tc, x_words, x_scales, w1, tab, offs, rel,
                 nc.scalar.activation(result[:], expd[b][:], ACT.Copy, scale=inverse)
             nc.sync.dma_start(out_rows[b], result[:])
 
-        bias0b = keep.tile([P, S // 2], F32, name="bias0b")
-        nc.vector.tensor_copy(bias0b[:], tabs[0][:].indirect(rel_sb[:, 16:32]))
         nc.vector.tensor_tensor(logits[0][:, KEYS_A], tabs[0][:].indirect(rel_sb[:, 0:16]), staged[0][:], ALU.add)
-        nc.vector.tensor_tensor(logits[0][:, KEYS_B], scores0b[:], bias0b[:], ALU.add)
-        nc.vector.tensor_tensor(logits[1][:, KEYS_A], tabs[1][:].indirect(rel_sb[:, 0:16]), staged[1][:], ALU.add)
-        nc.vector.tensor_tensor(logits[1][:, KEYS_B], tabs[1][:].indirect(rel_sb[:, 16:32]), staged1b[:], ALU.add)
-        exponentiate(0, "staged1")
-        add_bias(2)
-        normalise(0, invert(0), False)
-        exponentiate(1, "staged1")
-        add_bias(3)
+        add_bias(1)
+        nc.vector.tensor_tensor(logits[2][:, KEYS_A], tabs[2][:].indirect(rel_sb[:, 0:16]), staged[2][:], ALU.add)
+        nc.vector.tensor_tensor(logits[2][:, KEYS_B], tabs[2][:].indirect(rel_sb[:, 16:32]), staged2b[:], ALU.add)
+        exponentiate(1, "staged2")
+        exponentiate(0, "staged2b")
+        nc.vector.tensor_tensor(logits[3][:, KEYS_A], tabs[3][:].indirect(rel_sb[:, 0:16]), staged[3][:, KEYS_A], ALU.add)
         normalise(1, invert(1), False)
-        exponentiate(2, "staged1")
-        exponentiate(3, "logits1")
+        nc.vector.tensor_tensor(logits[3][:, KEYS_B], tabs[3][:].indirect(rel_sb[:, 16:32]), staged[3][:, KEYS_B], ALU.add)
+        normalise(0, invert(0), False)
+        exponentiate(2, "staged2b")
+        exponentiate(3, "logits0")
         inverse2 = invert(2)
         for name, keys in (("result2a", KEYS_A), ("result2b", KEYS_B)):
             piece = keep.tile([P, S // 2], F32, name=name)

@@ -41,7 +41,6 @@ def tile_picked_relbias_none_p_kernel(tc, x_words, x_scales, w1, tab, offs, rel,
         x_plane = keep.tile([P, S], U8, name="x_plane", align_bytes=64)
 
         nc.vector.memset(scale_table[:].bitcast(I32), 0)
-        nc.vector.memset(x_plane[:].bitcast(I32), 0)
         warm = keep.tile([P, 2], F32, name="warm")
         nc.vector.memset(warm[:, 0:1], 0.0)
         nc.scalar.activation(warm[:, 1:2], warm[:, 0:1], ACT.Exp)
@@ -52,7 +51,7 @@ def tile_picked_relbias_none_p_kernel(tc, x_words, x_scales, w1, tab, offs, rel,
         w_rows = w1.rearrange("(p j) c -> p j c", j=PACK)
         nc.sync.dma_start(w_raw[:, 0:1, :], w_rows[:, 0:1, :])
         nc.sync.dma_start(offs_sb[:], offs)
-        nc.sync.dma_start(scale_table[0:P:8, :].bitcast(I32), scale_rows)
+        nc.sync.dma_start(scale_table[4:P:8, :].bitcast(I32), scale_rows)
         nc.sync.dma_start(w_raw[:, 1:4, :], w_rows[:, 1:4, :])
         nc.sync.dma_start(word_table[:], x_words[0].rearrange("p c r -> p (c r)").bitcast(I32))
         nc.sync.dma_start(rel_sb[:], rel)
@@ -64,11 +63,13 @@ def tile_picked_relbias_none_p_kernel(tc, x_words, x_scales, w1, tab, offs, rel,
             nc.sync.dma_start(table[:], tab_rows[b])
             tabs.append(table)
 
+        load_tab(0, "tab0")
         x_bytes = keep.tile([P, S], U8, name="x_bytes", align_bytes=64)
         nc.vector.tensor_copy(x_bytes[:], scale_table[:].indirect(offs_sb[:]))
-        for r in range(4):
-            nc.sync.dma_start(x_plane[4 + r : P : 32, :].bitcast(I32), x_bytes[8 * r : P : 32, :].bitcast(I32))
-        load_tab(0, "scale_table")
+        nc.vector.tensor_copy(x_plane[:].bitcast(I32), x_bytes[:].bitcast(I32))
+        for r in range(1, 4):
+            nc.sync.dma_start(x_plane[4 + r : P : 32, :].bitcast(I32), x_bytes[4 + 8 * r : P : 32, :].bitcast(I32))
+        load_tab(1, "scale_table")
 
         grouped = [keep.tile([P, HALF, P, PACK], BF16, name=f"grouped{h}", align_bytes=64) for h in range(2)]
         dst = [grouped[h][:].rearrange("p b m j -> p m b j") for h in range(2)]
@@ -88,13 +89,12 @@ def tile_picked_relbias_none_p_kernel(tc, x_words, x_scales, w1, tab, offs, rel,
             w_codes.append(codes)
             w_bytes.append(scales)
 
-        load_tab(1, "w_raw")
-        load_tab(2, "grouped1")
+        load_tab(2, "w_raw")
+        load_tab(3, "grouped1")
 
         x_codes = keep.tile([P, S], U32, name="x_codes", align_bytes=64)
         for k in range(2):
             nc.vector.tensor_copy(x_codes[:, 256 * k : 256 * (k + 1)], word_table[:].bitcast(U32).indirect(offs_sb[:, 16 * k : 16 * (k + 1)]))
-        load_tab(3, "word_table")
 
         def score(b, keys, bank):
             h, cols = b // HALF, slice(P * (b % HALF), P * (b % HALF + 1))
@@ -110,19 +110,26 @@ def tile_picked_relbias_none_p_kernel(tc, x_words, x_scales, w1, tab, offs, rel,
             )
             return scores
 
-        staged = [keep.tile([P, S if b % 2 else S // 2], F32, name=f"staged{b}", align_bytes=64) for b in range(BLOCKS)]
+        staged = {b: keep.tile([P, S // 2 if b == 2 else S], F32, name=f"staged{b}", align_bytes=64) for b in (1, 2, 3)}
+        staged2b = keep.tile([P, S // 2], F32, name="staged2b", align_bytes=64)
         shared = keep.tile([P, S + S // 2], F32, name="shared", align_bytes=64)
-        logits = [keep.tile([P, S], F32, name="logits0", align_bytes=64), shared[:, S // 2 :], keep.tile([P, S], F32, name="logits2"), shared[:, :S]]
+        back = psum.tile([P, S], F32, name="back")
+        logits = [back, shared[:, S // 2 :], keep.tile([P, S], F32, name="logits2"), shared[:, :S]]
         expd, totals = {}, {}
 
-        nc.scalar.copy(staged[0][:], score(0, KEYS_A, "bank0a")[:])
-        nc.scalar.copy(staged[1][:, KEYS_A], score(1, KEYS_A, "bank1a")[:])
+        bias0 = keep.tile([P, S], F32, name="bias0")
+        nc.vector.tensor_copy(bias0[:], tabs[0][:].indirect(rel_sb[:]))
+        for keys, bank in ((slice(0, P), "bank1a"), (slice(P, 2 * P), "bank1c")):
+            nc.scalar.copy(staged[1][:, keys], score(1, keys, bank)[:])
         nc.scalar.copy(staged[1][:, KEYS_B], score(1, KEYS_B, "bank1b")[:])
-        scores0b = psum.tile([P, S // 2], F32, name="bank0b")
-        for k in range(2):
-            keys = slice(S // 2 + P * k, S // 2 + P * (k + 1))
+        scores2 = score(2, slice(0, S), "bank2")
+        nc.scalar.copy(staged[2][:], scores2[:, KEYS_A])
+        nc.scalar.copy(staged2b[:], scores2[:, KEYS_B])
+        scores0 = psum.tile([P, S], F32, name="bank0")
+        for k in range(4):
+            keys = slice(P * k, P * (k + 1))
             nc.tensor.matmul_mx(
-                out=scores0b[:, P * k : P * (k + 1)],
+                out=scores0[:, keys],
                 lhsT=x_codes[:, keys].bitcast(FP8X4),
                 lhsT_scale=x_plane[4:P, keys],
                 rhs=w_codes[0][:, 0:P].bitcast(FP8X4),
@@ -130,35 +137,26 @@ def tile_picked_relbias_none_p_kernel(tc, x_words, x_scales, w1, tab, offs, rel,
                 start=True,
                 stop=True,
             )
-        bias0b = keep.tile([P, S // 2], F32, name="bias0b")
-        nc.vector.tensor_copy(bias0b[:], tabs[0][:].indirect(rel_sb[:, 16:32]))
-        turned = psum.tile([P, S // 2], F32, name="turned")
-        for k in range(2):
-            nc.tensor.transpose(turned[:, P * k : P * (k + 1)], bias0b[:, P * k : P * (k + 1)], identity[:])
-        scores2 = score(2, slice(0, S), "bank2")
-        staged2b = keep.tile([P, S // 2], F32, name="staged2b", align_bytes=64)
-        nc.scalar.copy(staged[2][:], scores2[:, KEYS_A])
-        staged0b = keep.tile([P, S // 2], F32, name="staged0b")
-        nc.scalar.copy(staged0b[:], scores0b[:])
-        turned_sb = keep.tile([P, S // 2], F32, name="turned_sb")
-        nc.scalar.copy(turned_sb[:], turned[:])
-        nc.scalar.copy(staged2b[:], scores2[:, KEYS_B])
-        back = psum.tile([P, S // 2], F32, name="back")
-        for k in range(2):
+        staged0 = keep.tile([P, S], F32, name="staged0")
+        nc.scalar.copy(staged0[:], scores0[:])
+        turned_sb = keep.tile([P, S], F32, name="turned_sb")
+        for half, bank in enumerate(("bank1a", "bank1b")):
+            turned = psum.tile([P, S // 2], F32, name=bank)
+            for k in range(2):
+                cols = slice(P * (2 * half + k), P * (2 * half + k + 1))
+                nc.tensor.transpose(turned[:, P * k : P * (k + 1)], bias0[:, cols], identity[:])
+            nc.scalar.copy(turned_sb[:, 256 * half : 256 * (half + 1)], turned[:])
+        for k in range(4):
             cols = slice(P * k, P * (k + 1))
-            nc.tensor.matmul(back[:, cols], staged0b[:, cols], identity[:], start=True, stop=False, is_transpose=True)
+            nc.tensor.matmul(back[:, cols], staged0[:, cols], identity[:], start=True, stop=False, is_transpose=True)
             nc.tensor.matmul(back[:, cols], turned_sb[:, cols], identity[:], start=False, stop=True, is_transpose=True)
-        nc.scalar.copy(logits[0][:, KEYS_B], back[:])
-        nc.scalar.copy(staged[3][:], score(3, slice(0, S), "turned")[:])
-
-        def add_bias(b):
-            nc.vector.tensor_tensor(logits[b][:], tabs[b][:].indirect(rel_sb[:]), staged[b][:], ALU.add)
+        nc.scalar.copy(staged[3][:], score(3, slice(0, S), "bank3")[:])
 
         def exponentiate(b, tag):
             neg_max = keep.tile([P, 1], F32, name=tag, align_bytes=64)
             nc.vector.tensor_reduce(neg_max[:], logits[b][:], AX.X, ALU.max, negate=True)
             expd[b] = keep.tile([P, S], F32, name=f"expd{b}")
-            totals[b] = keep.tile([P, 1], F32, name=f"total{b}")
+            totals[b] = keep.tile([P, 1], F32, name=f"total{b}", align_bytes=64)
             nc.scalar.activation(expd[b][:], logits[b][:], ACT.Exp, bias=neg_max[:], scale=1.0, accum_out=totals[b][:])
 
         def invert(b):
@@ -174,8 +172,8 @@ def tile_picked_relbias_none_p_kernel(tc, x_words, x_scales, w1, tab, offs, rel,
                 nc.scalar.activation(result[:], expd[b][:], ACT.Copy, scale=inverse)
             nc.sync.dma_start(out_rows[b], result[:])
 
-        nc.vector.tensor_tensor(logits[0][:, KEYS_A], tabs[0][:].indirect(rel_sb[:, 0:16]), staged[0][:], ALU.add)
-        add_bias(1)
+        nc.vector.tensor_tensor(logits[1][:, KEYS_A], tabs[1][:].indirect(rel_sb[:, 0:16]), staged[1][:, KEYS_A], ALU.add)
+        nc.vector.tensor_tensor(logits[1][:, KEYS_B], tabs[1][:].indirect(rel_sb[:, 16:32]), staged[1][:, KEYS_B], ALU.add)
         nc.vector.tensor_tensor(logits[2][:, KEYS_A], tabs[2][:].indirect(rel_sb[:, 0:16]), staged[2][:], ALU.add)
         nc.vector.tensor_tensor(logits[2][:, KEYS_B], tabs[2][:].indirect(rel_sb[:, 16:32]), staged2b[:], ALU.add)
         exponentiate(1, "staged2")
@@ -185,7 +183,7 @@ def tile_picked_relbias_none_p_kernel(tc, x_words, x_scales, w1, tab, offs, rel,
         nc.vector.tensor_tensor(logits[3][:, KEYS_B], tabs[3][:].indirect(rel_sb[:, 16:32]), staged[3][:, KEYS_B], ALU.add)
         normalise(0, invert(0), False)
         exponentiate(2, "staged2b")
-        exponentiate(3, "logits0")
+        exponentiate(3, "total0")
         inverse2 = invert(2)
         for name, keys in (("result2a", KEYS_A), ("result2b", KEYS_B)):
             piece = keep.tile([P, S // 2], F32, name=name)

@@ -22,7 +22,7 @@ PACK = 4
 BLOCKS = N // P
 HALF = BLOCKS // 2
 KEYS_A, KEYS_B = slice(0, S // 2), slice(S // 2, S)
-CAST_SPLIT = 80
+CAST_SPLIT = 96
 TAIL_SPLIT = 256
 
 
@@ -49,10 +49,10 @@ def tile_picked_relbias_none_p_kernel(tc, x_words, x_scales, w1, tab, offs, rel,
         make_identity(nc, identity[:], nomemset=True)
         scale_rows = x_scales[0].bitcast(I32)
         w_rows = w1.rearrange("(p j) c -> p j c", j=PACK)
-        nc.sync.dma_start(w_raw[:, 0:1, :], w_rows[:, 0:1, :])
+        nc.sync.dma_start(w_raw[:, 0:2, :], w_rows[:, 0:2, :])
         nc.sync.dma_start(offs_sb[:], offs)
         nc.sync.dma_start(scale_table[4:P:8, :].bitcast(I32), scale_rows)
-        nc.sync.dma_start(w_raw[:, 1:4, :], w_rows[:, 1:4, :])
+        nc.sync.dma_start(w_raw[:, 2:4, :], w_rows[:, 2:4, :])
         nc.sync.dma_start(word_table[:], x_words[0].rearrange("p c r -> p (c r)").bitcast(I32))
         nc.sync.dma_start(rel_sb[:], rel)
         tab_rows = tab.rearrange("(p b) u -> b p u", b=BLOCKS)
@@ -110,8 +110,7 @@ def tile_picked_relbias_none_p_kernel(tc, x_words, x_scales, w1, tab, offs, rel,
             )
             return scores
 
-        staged = {b: keep.tile([P, S // 2 if b == 2 else S], F32, name=f"staged{b}", align_bytes=64) for b in (1, 2, 3)}
-        staged2b = keep.tile([P, S // 2], F32, name="staged2b", align_bytes=64)
+        staged = {b: keep.tile([P, S], F32, name=f"staged{b}", align_bytes=64) for b in (1, 2, 3)}
         shared = keep.tile([P, S + S // 2], F32, name="shared", align_bytes=64)
         back = psum.tile([P, S], F32, name="back")
         logits = [back, shared[:, S // 2 :], keep.tile([P, S], F32, name="logits2"), shared[:, :S]]
@@ -122,9 +121,7 @@ def tile_picked_relbias_none_p_kernel(tc, x_words, x_scales, w1, tab, offs, rel,
         for keys, bank in ((slice(0, P), "bank1a"), (slice(P, 2 * P), "bank1c")):
             nc.scalar.copy(staged[1][:, keys], score(1, keys, bank)[:])
         nc.scalar.copy(staged[1][:, KEYS_B], score(1, KEYS_B, "bank1b")[:])
-        scores2 = score(2, slice(0, S), "bank2")
-        nc.scalar.copy(staged[2][:], scores2[:, KEYS_A])
-        nc.scalar.copy(staged2b[:], scores2[:, KEYS_B])
+        nc.scalar.copy(staged[2][:], score(2, slice(0, S), "bank2")[:])
         scores0 = psum.tile([P, S], F32, name="bank0")
         for k in range(4):
             keys = slice(P * k, P * (k + 1))
@@ -152,12 +149,11 @@ def tile_picked_relbias_none_p_kernel(tc, x_words, x_scales, w1, tab, offs, rel,
             nc.tensor.matmul(back[:, cols], turned_sb[:, cols], identity[:], start=False, stop=True, is_transpose=True)
         nc.scalar.copy(staged[3][:], score(3, slice(0, S), "bank3")[:])
 
-        def exponentiate(b, tag):
-            neg_max = keep.tile([P, 1], F32, name=tag, align_bytes=64)
-            nc.vector.tensor_reduce(neg_max[:], logits[b][:], AX.X, ALU.max, negate=True)
+        def exponentiate(b, neg_max):
+            nc.vector.tensor_reduce(neg_max, logits[b][:], AX.X, ALU.max, negate=True)
             expd[b] = keep.tile([P, S], F32, name=f"expd{b}")
             totals[b] = keep.tile([P, 1], F32, name=f"total{b}", align_bytes=64)
-            nc.scalar.activation(expd[b][:], logits[b][:], ACT.Exp, bias=neg_max[:], scale=1.0, accum_out=totals[b][:])
+            nc.scalar.activation(expd[b][:], logits[b][:], ACT.Exp, bias=neg_max, scale=1.0, accum_out=totals[b][:])
 
         def invert(b):
             inverse = keep.tile([P, 1], F32, name=f"inverse{b}")
@@ -174,16 +170,16 @@ def tile_picked_relbias_none_p_kernel(tc, x_words, x_scales, w1, tab, offs, rel,
 
         nc.vector.tensor_tensor(logits[1][:, KEYS_A], tabs[1][:].indirect(rel_sb[:, 0:16]), staged[1][:, KEYS_A], ALU.add)
         nc.vector.tensor_tensor(logits[1][:, KEYS_B], tabs[1][:].indirect(rel_sb[:, 16:32]), staged[1][:, KEYS_B], ALU.add)
-        nc.vector.tensor_tensor(logits[2][:, KEYS_A], tabs[2][:].indirect(rel_sb[:, 0:16]), staged[2][:], ALU.add)
-        nc.vector.tensor_tensor(logits[2][:, KEYS_B], tabs[2][:].indirect(rel_sb[:, 16:32]), staged2b[:], ALU.add)
-        exponentiate(1, "staged2")
-        exponentiate(0, "staged2b")
+        nc.vector.tensor_tensor(logits[2][:, KEYS_A], tabs[2][:].indirect(rel_sb[:, 0:16]), staged[2][:, KEYS_A], ALU.add)
+        nc.vector.tensor_tensor(logits[2][:, KEYS_B], tabs[2][:].indirect(rel_sb[:, 16:32]), staged[2][:, KEYS_B], ALU.add)
+        exponentiate(1, staged[2][:, 0:1])
+        exponentiate(0, staged[2][:, S // 2 : S // 2 + 1])
         nc.vector.tensor_tensor(logits[3][:, KEYS_A], tabs[3][:].indirect(rel_sb[:, 0:16]), staged[3][:, KEYS_A], ALU.add)
         normalise(1, invert(1), False)
         nc.vector.tensor_tensor(logits[3][:, KEYS_B], tabs[3][:].indirect(rel_sb[:, 16:32]), staged[3][:, KEYS_B], ALU.add)
         normalise(0, invert(0), False)
-        exponentiate(2, "staged2b")
-        exponentiate(3, "total0")
+        exponentiate(2, staged[2][:, S // 2 : S // 2 + 1])
+        exponentiate(3, totals[0][:])
         inverse2 = invert(2)
         for name, keys in (("result2a", KEYS_A), ("result2b", KEYS_B)):
             piece = keep.tile([P, S // 2], F32, name=name)

@@ -163,7 +163,7 @@ def tile_picked_relbias_none_p_kernel(tc, x_words, x_scales, w1, tab, offs, rel,
         def normalise(b, inverse, on_vector):
             result = keep.tile([P, S], F32, name=f"result{b}")
             if on_vector:
-                nc.vector.tensor_scalar(result[:], expd[b][:], inverse, None, ALU.mult)
+                nc.gpsimd.tensor_scalar(result[:], expd[b][:], inverse, 0.0, ALU.mult, ALU.add)
             else:
                 nc.scalar.activation(result[:], expd[b][:], ACT.Copy, scale=inverse)
             nc.sync.dma_start(out_rows[b], result[:])
@@ -177,7 +177,7 @@ def tile_picked_relbias_none_p_kernel(tc, x_words, x_scales, w1, tab, offs, rel,
         nc.vector.tensor_tensor(logits[3][:, KEYS_A], tabs[3][:].indirect(rel_sb[:, 0:16]), staged[3][:, KEYS_A], ALU.add)
         normalise(1, invert(1), False)
         nc.vector.tensor_tensor(logits[3][:, KEYS_B], tabs[3][:].indirect(rel_sb[:, 16:32]), staged[3][:, KEYS_B], ALU.add)
-        normalise(0, invert(0), False)
+        normalise(0, invert(0), True)
         exponentiate(2, staged[2][:, S // 2 : S // 2 + 1])
         exponentiate(3, totals[0][:])
         inverse2 = invert(2)

@@ -22,7 +22,8 @@ PACK = 4
 BLOCKS = N // P
 HALF = BLOCKS // 2
 KEYS_A, KEYS_B = slice(0, S // 2), slice(S // 2, S)
-CAST_SPLIT = 96
+HEAD = 768
+CAST_SPLIT = 104
 TAIL_SPLIT = 256
 
 
@@ -48,11 +49,12 @@ def tile_picked_relbias_none_p_kernel(tc, x_words, x_scales, w1, tab, offs, rel,
         nc.vector.memset(identity[:], 0.0)
         make_identity(nc, identity[:], nomemset=True)
         scale_rows = x_scales[0].bitcast(I32)
-        w_rows = w1.rearrange("(p j) c -> p j c", j=PACK)
-        nc.sync.dma_start(w_raw[:, 0:2, :], w_rows[:, 0:2, :])
+        w_rows = w1.rearrange("(p j) c -> p (j c)", j=PACK)
+        w_flat = w_raw[:].rearrange("p j c -> p (j c)")
+        nc.sync.dma_start(w_flat[:, 0:HEAD], w_rows[:, 0:HEAD])
         nc.sync.dma_start(offs_sb[:], offs)
         nc.sync.dma_start(scale_table[4:P:8, :].bitcast(I32), scale_rows)
-        nc.sync.dma_start(w_raw[:, 2:4, :], w_rows[:, 2:4, :])
+        nc.sync.dma_start(w_flat[:, HEAD:], w_rows[:, HEAD:])
         nc.sync.dma_start(word_table[:], x_words[0].rearrange("p c r -> p (c r)").bitcast(I32))
         nc.sync.dma_start(rel_sb[:], rel)
         tab_rows = tab.rearrange("(p b) u -> b p u", b=BLOCKS)

@@ -1,7 +1,6 @@
 from contextlib import ExitStack
 
 import concourse.mybir as mybir
-from concourse.masks import make_identity
 
 K, T, S, N, U = 512, 2048, 512, 512, 1024
 FLOPS = 2 * K * N * S
@@ -45,9 +44,6 @@ def tile_picked_relbias_none_p_kernel(tc, x_words, x_scales, w1, tab, offs, rel,
         warm = keep.tile([P, 2], F32, name="warm")
         nc.vector.memset(warm[:, 0:1], 0.0)
         nc.scalar.activation(warm[:, 1:2], warm[:, 0:1], ACT.Exp)
-        identity = keep.tile([P, P], F32, name="identity")
-        nc.vector.memset(identity[:], 0.0)
-        make_identity(nc, identity[:], nomemset=True)
         scale_rows = x_scales[0].bitcast(I32)
         w_rows = w1.rearrange("(p j) c -> p (j c)", j=PACK)
         w_flat = w_raw[:].rearrange("p j c -> p (j c)")
@@ -112,76 +108,75 @@ def tile_picked_relbias_none_p_kernel(tc, x_words, x_scales, w1, tab, offs, rel,
             )
             return scores
 
-        staged = {b: keep.tile([P, S], F32, name=f"staged{b}", align_bytes=64) for b in (1, 2, 3)}
-        shared = keep.tile([P, S + S // 2], F32, name="shared", align_bytes=64)
-        back = psum.tile([P, S], F32, name="back")
-        logits = [back, shared[:, S // 2 :], keep.tile([P, S], F32, name="logits2"), shared[:, :S]]
+        logits = {b: keep.tile([P, S], F32, name=f"logits{b}") for b in (0, 2, 3)}
         expd, totals = {}, {}
 
-        bias0 = keep.tile([P, S], F32, name="bias0")
-        nc.vector.tensor_copy(bias0[:], tabs[0][:].indirect(rel_sb[:]))
-        for keys, bank in ((slice(0, P), "bank1a"), (slice(P, 2 * P), "bank1c")):
-            nc.scalar.copy(staged[1][:, keys], score(1, keys, bank)[:])
-        nc.scalar.copy(staged[1][:, KEYS_B], score(1, KEYS_B, "bank1b")[:])
-        nc.scalar.copy(staged[2][:], score(2, slice(0, S), "bank2")[:])
-        scores0 = psum.tile([P, S], F32, name="bank0")
-        for k in range(4):
-            keys = slice(P * k, P * (k + 1))
-            nc.tensor.matmul_mx(
-                out=scores0[:, keys],
-                lhsT=x_codes[:, keys].bitcast(FP8X4),
-                lhsT_scale=x_plane[4:P, keys],
-                rhs=w_codes[0][:, 0:P].bitcast(FP8X4),
-                rhs_scale=w_bytes[0][:, 0:P],
-                start=True,
-                stop=True,
-            )
-        staged0 = keep.tile([P, S], F32, name="staged0")
-        nc.scalar.copy(staged0[:], scores0[:])
-        turned_sb = keep.tile([P, S], F32, name="turned_sb")
-        for half, bank in enumerate(("bank1a", "bank1b")):
-            turned = psum.tile([P, S // 2], F32, name=bank)
-            for k in range(2):
-                cols = slice(P * (2 * half + k), P * (2 * half + k + 1))
-                nc.tensor.transpose(turned[:, P * k : P * (k + 1)], bias0[:, cols], identity[:])
-            nc.scalar.copy(turned_sb[:, 256 * half : 256 * (half + 1)], turned[:])
-        for k in range(4):
-            cols = slice(P * k, P * (k + 1))
-            nc.tensor.matmul(back[:, cols], staged0[:, cols], identity[:], start=True, stop=False, is_transpose=True)
-            nc.tensor.matmul(back[:, cols], turned_sb[:, cols], identity[:], start=False, stop=True, is_transpose=True)
-        nc.scalar.copy(staged[3][:], score(3, slice(0, S), "bank3")[:])
+        def offsets(keys):
+            return rel_sb[:, keys.start // 16 : keys.stop // 16]
 
-        def exponentiate(b, neg_max):
+        def fetch_on_scalar(b, keys):
+            bias = keep.tile([P, keys.stop - keys.start], F32, name=f"bias{b}", align_bytes=32)
+            nc.scalar.activation(bias[:], tabs[b][:].indirect(offsets(keys)), ACT.Copy)
+            return bias
+
+        def stage(b):
+            staged = keep.tile([P, S // 2], F32, name=f"staged{b}", align_bytes=32)
+            nc.scalar.copy(staged[:], score(b, KEYS_B, f"bank{b}b")[:])
+            return staged
+
+        def exponentiate(b, neg_max, tag=None):
             nc.vector.tensor_reduce(neg_max, logits[b][:], AX.X, ALU.max, negate=True)
-            expd[b] = keep.tile([P, S], F32, name=f"expd{b}")
+            expd[b] = tag if tag is not None else keep.tile([P, S], F32, name=f"expd{b}")
             totals[b] = keep.tile([P, 1], F32, name=f"total{b}", align_bytes=64)
             nc.scalar.activation(expd[b][:], logits[b][:], ACT.Exp, bias=neg_max, scale=1.0, accum_out=totals[b][:])
 
-        def invert(b):
-            inverse = keep.tile([P, 1], F32, name=f"inverse{b}")
-            nc.vector.reciprocal(inverse[:], totals[b][:])
-            return inverse[:]
+        def column(tag, align=32):
+            return keep.tile([P, 1], F32, name=tag, align_bytes=align)[:]
 
-        def normalise(b, inverse, on_vector):
+        def invert(b, tag=None):
+            inverse = column(tag or f"inverse{b}")
+            nc.vector.reciprocal(inverse, totals[b][:])
+            return inverse
+
+        def normalise(b, inverse, engine):
             result = keep.tile([P, S], F32, name=f"result{b}")
-            if on_vector:
-                nc.gpsimd.tensor_scalar(result[:], expd[b][:], inverse, 0.0, ALU.mult, ALU.add)
-            else:
-                nc.scalar.activation(result[:], expd[b][:], ACT.Copy, scale=inverse)
+            engine.tensor_scalar(result[:], expd[b][:], inverse, 0.0, ALU.mult, ALU.add)
             nc.sync.dma_start(out_rows[b], result[:])
 
-        nc.vector.tensor_tensor(logits[1][:, KEYS_A], tabs[1][:].indirect(rel_sb[:, 0:16]), staged[1][:, KEYS_A], ALU.add)
-        nc.vector.tensor_tensor(logits[1][:, KEYS_B], tabs[1][:].indirect(rel_sb[:, 16:32]), staged[1][:, KEYS_B], ALU.add)
-        nc.vector.tensor_tensor(logits[2][:, KEYS_A], tabs[2][:].indirect(rel_sb[:, 0:16]), staged[2][:, KEYS_A], ALU.add)
-        nc.vector.tensor_tensor(logits[2][:, KEYS_B], tabs[2][:].indirect(rel_sb[:, 16:32]), staged[2][:, KEYS_B], ALU.add)
-        exponentiate(1, staged[2][:, 0:1])
-        exponentiate(0, staged[2][:, S // 2 : S // 2 + 1])
-        nc.vector.tensor_tensor(logits[3][:, KEYS_A], tabs[3][:].indirect(rel_sb[:, 0:16]), staged[3][:, KEYS_A], ALU.add)
-        normalise(1, invert(1), False)
-        nc.vector.tensor_tensor(logits[3][:, KEYS_B], tabs[3][:].indirect(rel_sb[:, 16:32]), staged[3][:, KEYS_B], ALU.add)
-        normalise(0, invert(0), True)
-        exponentiate(2, staged[2][:, S // 2 : S // 2 + 1])
-        exponentiate(3, totals[0][:])
+        whole = slice(0, S)
+
+        def fetch_on_vector(b, keys, bias):
+            nc.vector.tensor_copy(bias, tabs[b][:].indirect(offsets(keys)))
+
+        def add(b, keys, scores, bias):
+            nc.vector.tensor_tensor(logits[b][:, keys], scores[:], bias, ALU.add)
+
+        bias0a = fetch_on_scalar(0, KEYS_A)
+        bias0b = keep.tile([P, S // 2], F32, name="bias0b")
+        fetch_on_vector(0, KEYS_B, bias0b[:])
+        add(0, KEYS_A, score(0, KEYS_A, "bank0a"), bias0a[:])
+        add(0, KEYS_B, score(0, KEYS_B, "bank0b"), bias0b[:])
+        bias1 = fetch_on_scalar(1, whole)
+        bias2 = keep.tile([P, S], F32, name="bias2", align_bytes=32)
+        nc.scalar.activation(bias2[:, KEYS_A], tabs[2][:].indirect(offsets(KEYS_A)), ACT.Copy)
+        neg_max0 = column("neg_max0")
+        nc.vector.tensor_reduce(neg_max0, logits[0][:], AX.X, ALU.max, negate=True)
+        fetch_on_vector(2, KEYS_B, bias2[:, KEYS_B])
+        after2 = keep.tile([P, 2 * S], F32, name="w_raw", align_bytes=64)
+        logits[1] = after2[:, 0:S]
+        expd[0] = after2[:, S:]
+        totals[0] = keep.tile([P, 1], F32, name="total0", align_bytes=64)
+        nc.scalar.activation(expd[0], logits[0][:], ACT.Exp, bias=neg_max0, scale=1.0, accum_out=totals[0][:])
+        add(1, whole, score(1, whole, "bank1"), bias1[:])
+        add(2, whole, score(2, whole, "bank2"), bias2[:])
+        bias3 = fetch_on_scalar(3, whole)
+        late = keep.tile([P, 2 * S], F32, name="grouped1", align_bytes=64)
+        exponentiate(1, column("neg_max1"), late[:, 0:S])
+        normalise(0, invert(0, "bias2"), nc.gpsimd)
+        exponentiate(2, column("neg_max2"), late[:, S:])
+        add(3, whole, score(3, whole, "bank3"), bias3[:])
+        normalise(1, invert(1), nc.gpsimd)
+        exponentiate(3, column("neg_max1"))
         inverse2 = invert(2)
         for name, keys in (("result2a", KEYS_A), ("result2b", KEYS_B)):
             piece = keep.tile([P, S // 2], F32, name=name)

@@ -20,10 +20,9 @@ P = 128
 PACK = 4
 BLOCKS = N // P
 HALF = BLOCKS // 2
-KEYS_A, KEYS_B = slice(0, S // 2), slice(S // 2, S)
+KEYS_A, KEYS_B, KEYS = slice(0, S // 2), slice(S // 2, S), slice(0, S)
 HEAD = 768
 CAST_SPLIT = 104
-TAIL_SPLIT = 256
 
 
 def tile_picked_relbias_none_p_kernel(tc, x_words, x_scales, w1, tab, offs, rel, out):
@@ -37,19 +36,18 @@ def tile_picked_relbias_none_p_kernel(tc, x_words, x_scales, w1, tab, offs, rel,
         scale_table = keep.tile([P, T], U8, name="scale_table", align_bytes=64)
         word_table = keep.tile([P, T], I32, name="word_table", align_bytes=64)
         w_raw = keep.tile([P, PACK, N], F32, name="w_raw", align_bytes=64)
-        tabs = []
         x_plane = keep.tile([P, S], U8, name="x_plane", align_bytes=64)
+        tabs = []
 
         nc.vector.memset(scale_table[:].bitcast(I32), 0)
         warm = keep.tile([P, 2], F32, name="warm")
         nc.vector.memset(warm[:, 0:1], 0.0)
         nc.scalar.activation(warm[:, 1:2], warm[:, 0:1], ACT.Exp)
-        scale_rows = x_scales[0].bitcast(I32)
         w_rows = w1.rearrange("(p j) c -> p (j c)", j=PACK)
         w_flat = w_raw[:].rearrange("p j c -> p (j c)")
         nc.sync.dma_start(w_flat[:, 0:HEAD], w_rows[:, 0:HEAD])
         nc.sync.dma_start(offs_sb[:], offs)
-        nc.sync.dma_start(scale_table[4:P:8, :].bitcast(I32), scale_rows)
+        nc.sync.dma_start(scale_table[4:P:8, :].bitcast(I32), x_scales[0].bitcast(I32))
         nc.sync.dma_start(w_flat[:, HEAD:], w_rows[:, HEAD:])
         nc.sync.dma_start(word_table[:], x_words[0].rearrange("p c r -> p (c r)").bitcast(I32))
         nc.sync.dma_start(rel_sb[:], rel)
@@ -91,8 +89,8 @@ def tile_picked_relbias_none_p_kernel(tc, x_words, x_scales, w1, tab, offs, rel,
         load_tab(3, "grouped1")
 
         x_codes = keep.tile([P, S], U32, name="x_codes", align_bytes=64)
-        for k in range(2):
-            nc.vector.tensor_copy(x_codes[:, 256 * k : 256 * (k + 1)], word_table[:].bitcast(U32).indirect(offs_sb[:, 16 * k : 16 * (k + 1)]))
+        for keys in (KEYS_A, KEYS_B):
+            nc.vector.tensor_copy(x_codes[:, keys], word_table[:].bitcast(U32).indirect(offs_sb[:, keys.start // 16 : keys.stop // 16]))
 
         def score(b, keys, bank):
             h, cols = b // HALF, slice(P * (b % HALF), P * (b % HALF + 1))
@@ -108,84 +106,73 @@ def tile_picked_relbias_none_p_kernel(tc, x_words, x_scales, w1, tab, offs, rel,
             )
             return scores
 
-        logits = {b: keep.tile([P, S], F32, name=f"logits{b}") for b in (0, 2, 3)}
-        expd, totals = {}, {}
+        def looked_up(b, keys):
+            return tabs[b][:].indirect(rel_sb[:, keys.start // 16 : keys.stop // 16])
 
-        def offsets(keys):
-            return rel_sb[:, keys.start // 16 : keys.stop // 16]
+        def wide(name, keys=KEYS, align=32):
+            return keep.tile([P, keys.stop - keys.start], F32, name=name, align_bytes=align)
+
+        def column(name, align=32):
+            return keep.tile([P, 1], F32, name=name, align_bytes=align)
+
+        logits = [wide(f"logits{b}") for b in range(BLOCKS)]
+        expd, totals, neg_max = {}, {}, {}
 
         def fetch_on_scalar(b, keys):
-            bias = keep.tile([P, keys.stop - keys.start], F32, name=f"bias{b}", align_bytes=32)
-            nc.scalar.activation(bias[:], tabs[b][:].indirect(offsets(keys)), ACT.Copy)
+            bias = wide(f"bias{b}", keys)
+            nc.scalar.activation(bias[:], looked_up(b, keys), ACT.Copy)
             return bias
 
-        def stage(b):
-            staged = keep.tile([P, S // 2], F32, name=f"staged{b}", align_bytes=32)
-            nc.scalar.copy(staged[:], score(b, KEYS_B, f"bank{b}b")[:])
-            return staged
+        def add(b, keys, scores, bias):
+            nc.vector.tensor_tensor(logits[b][:, keys], scores[:], bias[:], ALU.add)
 
-        def exponentiate(b, neg_max, tag=None):
-            nc.vector.tensor_reduce(neg_max, logits[b][:], AX.X, ALU.max, negate=True)
-            expd[b] = tag if tag is not None else keep.tile([P, S], F32, name=f"expd{b}")
-            totals[b] = keep.tile([P, 1], F32, name=f"total{b}", align_bytes=64)
-            nc.scalar.activation(expd[b][:], logits[b][:], ACT.Exp, bias=neg_max, scale=1.0, accum_out=totals[b][:])
+        def maximum(b, place):
+            neg_max[b] = place
+            nc.vector.tensor_reduce(neg_max[b][:], logits[b][:], AX.X, ALU.max, negate=True)
 
-        def column(tag, align=32):
-            return keep.tile([P, 1], F32, name=tag, align_bytes=align)[:]
+        def exponentiate(b, place):
+            expd[b] = place
+            totals[b] = column(f"total{b}", 64)
+            nc.scalar.activation(expd[b][:], logits[b][:], ACT.Exp, bias=neg_max[b][:], scale=1.0, accum_out=totals[b][:])
 
         def invert(b, tag=None):
             inverse = column(tag or f"inverse{b}")
-            nc.vector.reciprocal(inverse, totals[b][:])
+            nc.vector.reciprocal(inverse[:], totals[b][:])
             return inverse
 
-        def normalise(b, inverse, engine):
-            result = keep.tile([P, S], F32, name=f"result{b}")
-            engine.tensor_scalar(result[:], expd[b][:], inverse, 0.0, ALU.mult, ALU.add)
+        def normalise_on_gpsimd(b, inverse):
+            result = wide(f"result{b}")
+            nc.gpsimd.tensor_scalar(result[:], expd[b][:], inverse[:], 0.0, ALU.mult, ALU.add)
             nc.sync.dma_start(out_rows[b], result[:])
 
-        whole = slice(0, S)
-
-        def fetch_on_vector(b, keys, bias):
-            nc.vector.tensor_copy(bias, tabs[b][:].indirect(offsets(keys)))
-
-        def add(b, keys, scores, bias):
-            nc.vector.tensor_tensor(logits[b][:, keys], scores[:], bias, ALU.add)
-
         bias0a = fetch_on_scalar(0, KEYS_A)
-        bias0b = keep.tile([P, S // 2], F32, name="bias0b")
-        fetch_on_vector(0, KEYS_B, bias0b[:])
-        add(0, KEYS_A, score(0, KEYS_A, "bank0a"), bias0a[:])
-        add(0, KEYS_B, score(0, KEYS_B, "bank0b"), bias0b[:])
-        bias1 = fetch_on_scalar(1, whole)
-        bias2 = keep.tile([P, S], F32, name="bias2", align_bytes=32)
-        nc.scalar.activation(bias2[:, KEYS_A], tabs[2][:].indirect(offsets(KEYS_A)), ACT.Copy)
-        neg_max0 = column("neg_max0")
-        nc.vector.tensor_reduce(neg_max0, logits[0][:], AX.X, ALU.max, negate=True)
-        fetch_on_vector(2, KEYS_B, bias2[:, KEYS_B])
-        after2 = keep.tile([P, 2 * S], F32, name="w_raw", align_bytes=64)
-        logits[1] = after2[:, 0:S]
-        expd[0] = after2[:, S:]
-        totals[0] = keep.tile([P, 1], F32, name="total0", align_bytes=64)
-        nc.scalar.activation(expd[0], logits[0][:], ACT.Exp, bias=neg_max0, scale=1.0, accum_out=totals[0][:])
-        add(1, whole, score(1, whole, "bank1"), bias1[:])
-        add(2, whole, score(2, whole, "bank2"), bias2[:])
-        bias3 = fetch_on_scalar(3, whole)
-        late = keep.tile([P, 2 * S], F32, name="grouped1", align_bytes=64)
-        exponentiate(1, column("neg_max1"), late[:, 0:S])
-        normalise(0, invert(0, "bias2"), nc.gpsimd)
-        exponentiate(2, column("neg_max2"), late[:, S:])
-        add(3, whole, score(3, whole, "bank3"), bias3[:])
-        normalise(1, invert(1), nc.gpsimd)
-        exponentiate(3, column("neg_max1"))
-        inverse2 = invert(2)
-        for name, keys in (("result2a", KEYS_A), ("result2b", KEYS_B)):
-            piece = keep.tile([P, S // 2], F32, name=name)
-            nc.vector.tensor_scalar(piece[:], expd[2][:, keys], inverse2, None, ALU.mult)
-            nc.sync.dma_start(out_rows[2][:, keys], piece[:])
-        inverse = invert(3)
-        left = keep.tile([P, TAIL_SPLIT], F32, name="left")
-        right = keep.tile([P, S - TAIL_SPLIT], F32, name="right")
-        nc.vector.tensor_scalar(left[:], expd[3][:, 0:TAIL_SPLIT], inverse, None, ALU.mult)
-        nc.sync.dma_start(out_rows[3][:, 0:TAIL_SPLIT], left[:])
-        nc.scalar.activation(right[:], expd[3][:, TAIL_SPLIT:S], ACT.Copy, scale=inverse)
-        nc.scalar.dma_start(out_rows[3][:, TAIL_SPLIT:S], right[:])
+        bias0b = wide("bias0b", KEYS_B)
+        nc.vector.tensor_copy(bias0b[:], looked_up(0, KEYS_B))
+        add(0, KEYS_A, score(0, KEYS_A, "bank0a"), bias0a)
+        add(0, KEYS_B, score(0, KEYS_B, "bank0b"), bias0b)
+        bias1 = fetch_on_scalar(1, KEYS)
+        maximum(0, column("shared_max"))
+        add(1, KEYS, score(1, KEYS, "bank1"), bias1)
+        exponentiate(0, wide("expd0"))
+        bias2 = wide("bias2")
+        nc.vector.tensor_copy(bias2[:, KEYS_B], looked_up(2, KEYS_B))
+        nc.scalar.activation(bias2[:, KEYS_A], looked_up(2, KEYS_A), ACT.Copy)
+        maximum(1, column("shared_max"))
+        add(2, KEYS, score(2, KEYS, "bank2"), bias2)
+        normalise_on_gpsimd(0, invert(0, "bias2"))
+        bias3 = fetch_on_scalar(3, KEYS)
+        after_tab3 = keep.tile([P, S + 8], F32, name="grouped1", align_bytes=64)
+        exponentiate(1, after_tab3[:, 0:S])
+        add(3, KEYS, score(3, KEYS, "bank3"), bias3)
+        maximum(2, after_tab3[:, S : S + 1])
+        exponentiate(2, wide("expd2"))
+        normalise_on_gpsimd(1, invert(1))
+        maximum(3, column("neg_max3"))
+        exponentiate(3, wide("expd3"))
+        for b in (2, 3):
+            inverse = invert(b)
+            left, right = wide(f"left{b}", KEYS_A), wide(f"right{b}", KEYS_B)
+            nc.vector.tensor_scalar(left[:], expd[b][:, KEYS_A], inverse[:], None, ALU.mult)
+            nc.sync.dma_start(out_rows[b][:, KEYS_A], left[:])
+            nc.scalar.activation(right[:], expd[b][:, KEYS_B], ACT.Copy, scale=inverse[:])
+            (nc.sync if b == 2 else nc.scalar).dma_start(out_rows[b][:, KEYS_B], right[:])

@@ -151,27 +151,27 @@ def tile_picked_relbias_none_p_kernel(tc, x_words, x_scales, w1, tab, offs, rel,
         add(0, KEYS_A, score(0, KEYS_A, "bank0a"), bias0a)
         add(0, KEYS_B, score(0, KEYS_B, "bank0b"), bias0b)
         bias1 = fetch_on_scalar(1, KEYS)
-        maximum(0, column("shared_max"))
+        maximum(0, column("neg_max0"))
         add(1, KEYS, score(1, KEYS, "bank1"), bias1)
-        exponentiate(0, wide("expd0"))
-        bias2 = wide("bias2")
-        nc.vector.tensor_copy(bias2[:, KEYS_B], looked_up(2, KEYS_B))
-        nc.scalar.activation(bias2[:, KEYS_A], looked_up(2, KEYS_A), ACT.Copy)
-        maximum(1, column("shared_max"))
+        bias2 = fetch_on_scalar(2, KEYS)
+        exponentiate(0, wide("bias1"))
+        maximum(1, column("neg_max1"))
         add(2, KEYS, score(2, KEYS, "bank2"), bias2)
-        normalise_on_gpsimd(0, invert(0, "bias2"))
-        bias3 = fetch_on_scalar(3, KEYS)
-        after_tab3 = keep.tile([P, S + 8], F32, name="grouped1", align_bytes=64)
-        exponentiate(1, after_tab3[:, 0:S])
-        add(3, KEYS, score(3, KEYS, "bank3"), bias3)
-        maximum(2, after_tab3[:, S : S + 1])
+        bias3 = wide("bias3")
+        for keys in (KEYS_A, KEYS_B):
+            nc.scalar.activation(bias3[:, keys], looked_up(3, keys), ACT.Copy)
+        normalise_on_gpsimd(0, invert(0))
+        exponentiate(1, wide("bias2"))
+        maximum(2, column("neg_max2"))
+        add(3, KEYS_A, score(3, KEYS_A, "bank3a"), bias3[:, KEYS_A])
+        add(3, KEYS_B, score(3, KEYS_B, "bank3b"), bias3[:, KEYS_B])
         exponentiate(2, wide("expd2"))
         normalise_on_gpsimd(1, invert(1))
         maximum(3, column("neg_max3"))
         exponentiate(3, wide("expd3"))
         for b in (2, 3):
             inverse = invert(b)
-            left, right = wide(f"left{b}", KEYS_A), wide(f"right{b}", KEYS_B)
+            left, right = wide(f"left{b}", KEYS_A), wide("logits3" if b == 2 else "right3", KEYS_B)
             nc.vector.tensor_scalar(left[:], expd[b][:, KEYS_A], inverse[:], None, ALU.mult)
             nc.sync.dma_start(out_rows[b][:, KEYS_A], left[:])
             nc.scalar.activation(right[:], expd[b][:, KEYS_B], ACT.Copy, scale=inverse[:])

@@ -21,7 +21,7 @@ PACK = 4
 BLOCKS = N // P
 HALF = BLOCKS // 2
 KEYS_A, KEYS_B, KEYS = slice(0, S // 2), slice(S // 2, S), slice(0, S)
-HEAD = 768
+HEAD = 640
 CAST_SPLIT = 104
 
 
@@ -29,19 +29,22 @@ def tile_picked_relbias_none_p_kernel(tc, x_words, x_scales, w1, tab, offs, rel,
     nc = tc.nc
     with ExitStack() as ctx:
         keep = ctx.enter_context(tc.tile_pool(name="keep", bufs=1))
+        early = ctx.enter_context(tc.tile_pool(name="early", bufs=1))
         psum = ctx.enter_context(tc.psum_pool(name="psum", bufs=1))
 
         offs_sb = keep.tile([P, S // 16], U16, name="offs_sb")
         rel_sb = keep.tile([P, S // 16], U16, name="rel_sb")
-        scale_table = keep.tile([P, T], U8, name="scale_table", align_bytes=64)
+        scale_table = early.tile([P, T], U8, name="scale_table", align_bytes=64, offset=4 * U - T // 2)
         word_table = keep.tile([P, T], I32, name="word_table", align_bytes=64)
         w_raw = keep.tile([P, PACK, N], F32, name="w_raw", align_bytes=64)
         x_plane = keep.tile([P, S], U8, name="x_plane", align_bytes=64)
         tabs = []
 
-        nc.vector.memset(scale_table[:].bitcast(I32), 0)
+        nc.vector.memset(scale_table[:, 0:1280].bitcast(I32), 0)
+        nc.gpsimd.memset(scale_table[:, 1280:T].bitcast(I32), 0)
         warm = keep.tile([P, 2], F32, name="warm")
         nc.vector.memset(warm[:, 0:1], 0.0)
+        nc.vector.memset(x_plane[:].bitcast(I32), 0)
         nc.scalar.activation(warm[:, 1:2], warm[:, 0:1], ACT.Exp)
         w_rows = w1.rearrange("(p j) c -> p (j c)", j=PACK)
         w_flat = w_raw[:].rearrange("p j c -> p (j c)")
@@ -59,13 +62,15 @@ def tile_picked_relbias_none_p_kernel(tc, x_words, x_scales, w1, tab, offs, rel,
             nc.sync.dma_start(table[:], tab_rows[b])
             tabs.append(table)
 
-        load_tab(0, "tab0")
         x_bytes = keep.tile([P, S], U8, name="x_bytes", align_bytes=64)
         nc.vector.tensor_copy(x_bytes[:], scale_table[:].indirect(offs_sb[:]))
-        nc.vector.tensor_copy(x_plane[:].bitcast(I32), x_bytes[:].bitcast(I32))
-        for r in range(1, 4):
-            nc.sync.dma_start(x_plane[4 + r : P : 32, :].bitcast(I32), x_bytes[4 + 8 * r : P : 32, :].bitcast(I32))
-        load_tab(1, "scale_table")
+        for r in range(4):
+            queue = nc.sync if r < 2 else nc.scalar
+            queue.dma_start(x_plane[4 + r : P : 32, :].bitcast(I32), x_bytes[4 + 8 * r : P : 32, :].bitcast(I32))
+        for b in range(2):
+            table = early.tile([P, U], F32, name=f"tab{b}", align_bytes=64, offset=4 * U * b)
+            nc.sync.dma_start(table[:], tab_rows[b])
+            tabs.append(table)
 
         grouped = [keep.tile([P, HALF, P, PACK], BF16, name=f"grouped{h}", align_bytes=64) for h in range(2)]
         dst = [grouped[h][:].rearrange("p b m j -> p m b j") for h in range(2)]
@@ -145,34 +150,51 @@ def tile_picked_relbias_none_p_kernel(tc, x_words, x_scales, w1, tab, offs, rel,
             nc.gpsimd.tensor_scalar(result[:], expd[b][:], inverse[:], 0.0, ALU.mult, ALU.add)
             nc.sync.dma_start(out_rows[b], result[:])
 
+        y0a = score(0, KEYS_A, "bank0a")
+        y2a = score(2, KEYS_A, "bank2a")
+        y0b = score(0, KEYS_B, "bank0b")
+        y1 = score(1, KEYS, "bank1")
         bias0a = fetch_on_scalar(0, KEYS_A)
         bias0b = wide("bias0b", KEYS_B)
         nc.vector.tensor_copy(bias0b[:], looked_up(0, KEYS_B))
-        add(0, KEYS_A, score(0, KEYS_A, "bank0a"), bias0a)
-        add(0, KEYS_B, score(0, KEYS_B, "bank0b"), bias0b)
-        bias1 = fetch_on_scalar(1, KEYS)
+        add(0, KEYS_A, y0a, bias0a)
+        add(0, KEYS_B, y0b, bias0b)
+        staged = early.tile([P, S // 2], F32, name="staged", align_bytes=64, offset=0)
+        nc.scalar.copy(staged[:], y2a[:])
+        shared = keep.tile([P, S + S // 2], F32, name="shared")
+        bias1 = shared[:, S // 2 :]
+        nc.scalar.activation(bias1, looked_up(1, KEYS), ACT.Copy)
+        y2b = score(2, KEYS_B, "bank2b")
+        y3a = score(3, KEYS_A, "bank3a")
+        y3b = score(3, KEYS_B, "bank3b")
         maximum(0, column("neg_max0"))
-        add(1, KEYS, score(1, KEYS, "bank1"), bias1)
-        bias2 = fetch_on_scalar(2, KEYS)
-        exponentiate(0, wide("bias1"))
-        maximum(1, column("neg_max1"))
-        add(2, KEYS, score(2, KEYS, "bank2"), bias2)
+        add(1, KEYS_A, y1[:, KEYS_A], bias1[:, KEYS_A])
+        add(1, KEYS_B, y1[:, KEYS_B], bias1[:, KEYS_B])
+        bias2b = fetch_on_scalar(2, KEYS_B)
+        nc.vector.tensor_tensor(logits[2][:, KEYS_A], looked_up(2, KEYS_A), staged[:], ALU.add)
+        exponentiate(0, shared[:, 0:S])
+        add(2, KEYS_B, y2b, bias2b)
+        maximum(1, column("w_raw", 64))
         bias3 = wide("bias3")
         for keys in (KEYS_A, KEYS_B):
             nc.scalar.activation(bias3[:, keys], looked_up(3, keys), ACT.Copy)
-        normalise_on_gpsimd(0, invert(0))
-        exponentiate(1, wide("bias2"))
+        normalise_on_gpsimd(0, invert(0, "bias2"))
+        exponentiate(1, wide("expd1"))
         maximum(2, column("neg_max2"))
-        add(3, KEYS_A, score(3, KEYS_A, "bank3a"), bias3[:, KEYS_A])
-        add(3, KEYS_B, score(3, KEYS_B, "bank3b"), bias3[:, KEYS_B])
+        add(3, KEYS_A, y3a, bias3[:, KEYS_A])
+        add(3, KEYS_B, y3b, bias3[:, KEYS_B])
         exponentiate(2, wide("expd2"))
         normalise_on_gpsimd(1, invert(1))
-        maximum(3, column("neg_max3"))
+        maximum(3, column("w_raw", 64))
         exponentiate(3, wide("expd3"))
-        for b in (2, 3):
-            inverse = invert(b)
-            left, right = wide(f"left{b}", KEYS_A), wide("logits3" if b == 2 else "right3", KEYS_B)
-            nc.vector.tensor_scalar(left[:], expd[b][:, KEYS_A], inverse[:], None, ALU.mult)
-            nc.sync.dma_start(out_rows[b][:, KEYS_A], left[:])
-            nc.scalar.activation(right[:], expd[b][:, KEYS_B], ACT.Copy, scale=inverse[:])
-            (nc.sync if b == 2 else nc.scalar).dma_start(out_rows[b][:, KEYS_B], right[:])
+        inverse2 = invert(2)
+        for name, keys in (("result2a", KEYS_A), ("result2b", KEYS_B)):
+            piece = wide(name, keys)
+            nc.vector.tensor_scalar(piece[:], expd[2][:, keys], inverse2[:], None, ALU.mult)
+            nc.sync.dma_start(out_rows[2][:, keys], piece[:])
+        inverse3 = invert(3)
+        left, right = wide("left", KEYS_A), wide("right", KEYS_B)
+        nc.vector.tensor_scalar(left[:], expd[3][:, KEYS_A], inverse3[:], None, ALU.mult)
+        nc.sync.dma_start(out_rows[3][:, KEYS_A], left[:])
+        nc.scalar.activation(right[:], expd[3][:, KEYS_B], ACT.Copy, scale=inverse3[:])
+        nc.scalar.dma_start(out_rows[3][:, KEYS_B], right[:])

@@ -65,8 +65,7 @@ def tile_picked_relbias_none_p_kernel(tc, x_words, x_scales, w1, tab, offs, rel,
         x_bytes = keep.tile([P, S], U8, name="x_bytes", align_bytes=64)
         nc.vector.tensor_copy(x_bytes[:], scale_table[:].indirect(offs_sb[:]))
         for r in range(4):
-            queue = nc.sync if r < 2 else nc.scalar
-            queue.dma_start(x_plane[4 + r : P : 32, :].bitcast(I32), x_bytes[4 + 8 * r : P : 32, :].bitcast(I32))
+            nc.sync.dma_start(x_plane[4 + r : P : 32, :].bitcast(I32), x_bytes[4 + 8 * r : P : 32, :].bitcast(I32))
         for b in range(2):
             table = early.tile([P, U], F32, name=f"tab{b}", align_bytes=64, offset=4 * U * b)
             nc.sync.dma_start(table[:], tab_rows[b])

@@ -21,7 +21,7 @@ PACK = 4
 BLOCKS = N // P
 HALF = BLOCKS // 2
 KEYS_A, KEYS_B, KEYS = slice(0, S // 2), slice(S // 2, S), slice(0, S)
-HEAD = 640
+HEAD = 576
 CAST_SPLIT = 104
 
 
@@ -40,8 +40,8 @@ def tile_picked_relbias_none_p_kernel(tc, x_words, x_scales, w1, tab, offs, rel,
         x_plane = keep.tile([P, S], U8, name="x_plane", align_bytes=64)
         tabs = []
 
-        nc.vector.memset(scale_table[:, 0:1280].bitcast(I32), 0)
-        nc.gpsimd.memset(scale_table[:, 1280:T].bitcast(I32), 0)
+        nc.vector.memset(scale_table[:, 0:1024].bitcast(I32), 0)
+        nc.gpsimd.memset(scale_table[:, 1024:T].bitcast(I32), 0)
         warm = keep.tile([P, 2], F32, name="warm")
         nc.vector.memset(warm[:, 0:1], 0.0)
         nc.vector.memset(x_plane[:].bitcast(I32), 0)
@@ -149,6 +149,8 @@ def tile_picked_relbias_none_p_kernel(tc, x_words, x_scales, w1, tab, offs, rel,
             nc.gpsimd.tensor_scalar(result[:], expd[b][:], inverse[:], 0.0, ALU.mult, ALU.add)
             nc.sync.dma_start(out_rows[b], result[:])
 
+        minus_one = column("minus_one")
+        nc.vector.memset(minus_one[:], -1.0)
         y0a = score(0, KEYS_A, "bank0a")
         y2a = score(2, KEYS_A, "bank2a")
         y0b = score(0, KEYS_B, "bank0b")
@@ -177,7 +179,9 @@ def tile_picked_relbias_none_p_kernel(tc, x_words, x_scales, w1, tab, offs, rel,
         bias3 = wide("bias3")
         for keys in (KEYS_A, KEYS_B):
             nc.scalar.activation(bias3[:, keys], looked_up(3, keys), ACT.Copy)
-        normalise_on_gpsimd(0, invert(0, "bias2"))
+        inverse0 = column("inverse0")
+        nc.gpsimd.tensor_tensor(inverse0[:], totals[0][:], minus_one[:], ALU.pow)
+        normalise_on_gpsimd(0, inverse0)
         exponentiate(1, wide("expd1"))
         maximum(2, column("neg_max2"))
         add(3, KEYS_A, y3a, bias3[:, KEYS_A])

from contextlib import ExitStack

import concourse.mybir as mybir

K, T, S, N, U = 512, 2048, 512, 512, 1024
FLOPS = 2 * K * N * S

F32 = mybir.dt.float32
BF16 = mybir.dt.bfloat16
I32 = mybir.dt.int32
U32 = mybir.dt.uint32
U16 = mybir.dt.uint16
U8 = mybir.dt.uint8
FP8X4 = mybir.dt.float8_e4m3fn_x4
ALU = mybir.AluOpType
ACT = mybir.ActivationFunctionType
AX = mybir.AxisListType

P = 128
PACK = 4
BLOCKS = N // P
HALF = BLOCKS // 2
KEYS_A, KEYS_B, KEYS = slice(0, S // 2), slice(S // 2, S), slice(0, S)
HEAD = 576
CAST_SPLIT = 104


def tile_picked_relbias_none_p_kernel(tc, x_words, x_scales, w1, tab, offs, rel, out):
    nc = tc.nc
    with ExitStack() as ctx:
        keep = ctx.enter_context(tc.tile_pool(name="keep", bufs=1))
        early = ctx.enter_context(tc.tile_pool(name="early", bufs=1))
        psum = ctx.enter_context(tc.psum_pool(name="psum", bufs=1))

        offs_sb = keep.tile([P, S // 16], U16, name="offs_sb")
        rel_sb = keep.tile([P, S // 16], U16, name="rel_sb")
        scale_table = early.tile([P, T], U8, name="scale_table", align_bytes=64, offset=4 * U - T // 2)
        word_table = keep.tile([P, T], I32, name="word_table", align_bytes=64)
        w_raw = keep.tile([P, PACK, N], F32, name="w_raw", align_bytes=64)
        x_plane = keep.tile([P, S], U8, name="x_plane", align_bytes=64)
        tabs = []

        nc.vector.memset(scale_table[:, 0:1024].bitcast(I32), 0)
        nc.gpsimd.memset(scale_table[:, 1024:T].bitcast(I32), 0)
        warm = keep.tile([P, 2], F32, name="warm")
        nc.vector.memset(warm[:, 0:1], 0.0)
        nc.vector.memset(x_plane[:].bitcast(I32), 0)
        nc.scalar.activation(warm[:, 1:2], warm[:, 0:1], ACT.Exp)
        w_rows = w1.rearrange("(p j) c -> p (j c)", j=PACK)
        w_flat = w_raw[:].rearrange("p j c -> p (j c)")
        nc.sync.dma_start(w_flat[:, 0:HEAD], w_rows[:, 0:HEAD])
        nc.sync.dma_start(offs_sb[:], offs)
        nc.sync.dma_start(scale_table[4:P:8, :].bitcast(I32), x_scales[0].bitcast(I32))
        nc.sync.dma_start(w_flat[:, HEAD:], w_rows[:, HEAD:])
        nc.sync.dma_start(word_table[:], x_words[0].rearrange("p c r -> p (c r)").bitcast(I32))
        nc.sync.dma_start(rel_sb[:], rel)
        tab_rows = tab.rearrange("(p b) u -> b p u", b=BLOCKS)
        out_rows = out.rearrange("(p b) s -> b p s", b=BLOCKS)

        def load_tab(b, tag):
            table = keep.tile([P, U], F32, name=tag, align_bytes=64)
            nc.sync.dma_start(table[:], tab_rows[b])
            tabs.append(table)

        x_bytes = keep.tile([P, S], U8, name="x_bytes", align_bytes=64)
        nc.vector.tensor_copy(x_bytes[:], scale_table[:].indirect(offs_sb[:]))
        for r in range(4):
            nc.sync.dma_start(x_plane[4 + r : P : 32, :].bitcast(I32), x_bytes[4 + 8 * r : P : 32, :].bitcast(I32))
        for b in range(2):
            table = early.tile([P, U], F32, name=f"tab{b}", align_bytes=64, offset=4 * U * b)
            nc.sync.dma_start(table[:], tab_rows[b])
            tabs.append(table)

        grouped = [keep.tile([P, HALF, P, PACK], BF16, name=f"grouped{h}", align_bytes=64) for h in range(2)]
        dst = [grouped[h][:].rearrange("p b m j -> p m b j") for h in range(2)]
        src = w_raw[:].rearrange("p j (m b) -> p m b j", b=BLOCKS)
        nc.vector.tensor_copy(dst[0], src[:, :, 0:HALF])
        nc.scalar.activation(dst[1][:, 0:CAST_SPLIT], src[:, 0:CAST_SPLIT, HALF:BLOCKS], ACT.Copy)
        nc.vector.tensor_copy(dst[1][:, CAST_SPLIT:P], src[:, CAST_SPLIT:P, HALF:BLOCKS])
        w_codes, w_bytes = [], []
        for h in range(2):
            codes = keep.tile([P, HALF * P], U32, name=f"w_codes{h}", align_bytes=64)
            scales = keep.tile([P, HALF * P], U8, name=f"w_bytes{h}", align_bytes=64)
            nc.vector.quantize_mx(
                out=codes[:].bitcast(FP8X4),
                scales=scales[:],
                in_=grouped[h][:].rearrange("p b m j -> p (b m j)"),
            )
            w_codes.append(codes)
            w_bytes.append(scales)

        load_tab(2, "w_raw")
        load_tab(3, "grouped1")

        x_codes = keep.tile([P, S], U32, name="x_codes", align_bytes=64)
        for keys in (KEYS_A, KEYS_B):
            nc.vector.tensor_copy(x_codes[:, keys], word_table[:].bitcast(U32).indirect(offs_sb[:, keys.start // 16 : keys.stop // 16]))

        def score(b, keys, bank):
            h, cols = b // HALF, slice(P * (b % HALF), P * (b % HALF + 1))
            scores = psum.tile([P, keys.stop - keys.start], F32, name=bank)
            nc.tensor.matmul_mx(
                out=scores[:],
                lhsT=w_codes[h][:, cols].bitcast(FP8X4),
                lhsT_scale=w_bytes[h][:, cols],
                rhs=x_codes[:, keys].bitcast(FP8X4),
                rhs_scale=x_plane[4:P, keys],
                start=True,
                stop=True,
            )
            return scores

        def looked_up(b, keys):
            return tabs[b][:].indirect(rel_sb[:, keys.start // 16 : keys.stop // 16])

        def wide(name, keys=KEYS, align=32):
            return keep.tile([P, keys.stop - keys.start], F32, name=name, align_bytes=align)

        def column(name, align=32):
            return keep.tile([P, 1], F32, name=name, align_bytes=align)

        logits = [wide(f"logits{b}") for b in range(BLOCKS)]
        expd, totals, neg_max = {}, {}, {}

        def fetch_on_scalar(b, keys):
            bias = wide(f"bias{b}", keys)
            nc.scalar.activation(bias[:], looked_up(b, keys), ACT.Copy)
            return bias

        def add(b, keys, scores, bias):
            nc.vector.tensor_tensor(logits[b][:, keys], scores[:], bias[:], ALU.add)

        def maximum(b, place):
            neg_max[b] = place
            nc.vector.tensor_reduce(neg_max[b][:], logits[b][:], AX.X, ALU.max, negate=True)

        def exponentiate(b, place):
            expd[b] = place
            totals[b] = column(f"total{b}", 64)
            nc.scalar.activation(expd[b][:], logits[b][:], ACT.Exp, bias=neg_max[b][:], scale=1.0, accum_out=totals[b][:])

        def invert(b, tag=None):
            inverse = column(tag or f"inverse{b}")
            nc.vector.reciprocal(inverse[:], totals[b][:])
            return inverse

        def normalise_on_gpsimd(b, inverse):
            result = wide(f"result{b}")
            nc.gpsimd.tensor_scalar(result[:], expd[b][:], inverse[:], 0.0, ALU.mult, ALU.add)
            nc.sync.dma_start(out_rows[b], result[:])

        minus_one = column("minus_one")
        nc.vector.memset(minus_one[:], -1.0)
        y0a = score(0, KEYS_A, "bank0a")
        y2a = score(2, KEYS_A, "bank2a")
        y0b = score(0, KEYS_B, "bank0b")
        y1 = score(1, KEYS, "bank1")
        bias0a = fetch_on_scalar(0, KEYS_A)
        bias0b = wide("bias0b", KEYS_B)
        nc.vector.tensor_copy(bias0b[:], looked_up(0, KEYS_B))
        add(0, KEYS_A, y0a, bias0a)
        add(0, KEYS_B, y0b, bias0b)
        staged = early.tile([P, S // 2], F32, name="staged", align_bytes=64, offset=0)
        nc.scalar.copy(staged[:], y2a[:])
        shared = keep.tile([P, S + S // 2], F32, name="shared")
        bias1 = shared[:, S // 2 :]
        nc.scalar.activation(bias1, looked_up(1, KEYS), ACT.Copy)
        y2b = score(2, KEYS_B, "bank2b")
        y3a = score(3, KEYS_A, "bank3a")
        y3b = score(3, KEYS_B, "bank3b")
        maximum(0, column("neg_max0"))
        add(1, KEYS_A, y1[:, KEYS_A], bias1[:, KEYS_A])
        add(1, KEYS_B, y1[:, KEYS_B], bias1[:, KEYS_B])
        bias2b = fetch_on_scalar(2, KEYS_B)
        nc.vector.tensor_tensor(logits[2][:, KEYS_A], looked_up(2, KEYS_A), staged[:], ALU.add)
        exponentiate(0, shared[:, 0:S])
        add(2, KEYS_B, y2b, bias2b)
        maximum(1, column("w_raw", 64))
        bias3 = wide("bias3")
        for keys in (KEYS_A, KEYS_B):
            nc.scalar.activation(bias3[:, keys], looked_up(3, keys), ACT.Copy)
        inverse0 = column("inverse0")
        nc.gpsimd.tensor_tensor(inverse0[:], totals[0][:], minus_one[:], ALU.pow)
        normalise_on_gpsimd(0, inverse0)
        exponentiate(1, wide("expd1"))
        maximum(2, column("neg_max2"))
        add(3, KEYS_A, y3a, bias3[:, KEYS_A])
        add(3, KEYS_B, y3b, bias3[:, KEYS_B])
        exponentiate(2, wide("expd2"))
        normalise_on_gpsimd(1, invert(1))
        maximum(3, column("w_raw", 64))
        exponentiate(3, wide("expd3"))
        inverse2 = invert(2)
        for name, keys in (("result2a", KEYS_A), ("result2b", KEYS_B)):
            piece = wide(name, keys)
            nc.vector.tensor_scalar(piece[:], expd[2][:, keys], inverse2[:], None, ALU.mult)
            nc.sync.dma_start(out_rows[2][:, keys], piece[:])
        inverse3 = invert(3)
        left, right = wide("left", KEYS_A), wide("right", KEYS_B)
        nc.vector.tensor_scalar(left[:], expd[3][:, KEYS_A], inverse3[:], None, ALU.mult)
        nc.sync.dma_start(out_rows[3][:, KEYS_A], left[:])
        nc.scalar.activation(right[:], expd[3][:, KEYS_B], ACT.Copy, scale=inverse3[:])
        nc.scalar.dma_start(out_rows[3][:, KEYS_B], right[:])
